import numpy as np
import ml_dtypes


def mxq(x, axis, fmt="e4m3"):
    dtype, down = {"e4m3": (ml_dtypes.float8_e4m3fn, 7), "e5m2": (ml_dtypes.float8_e5m2, 14)}[fmt]
    v = np.moveaxis(np.asarray(x, np.float32).astype(ml_dtypes.bfloat16).astype(np.float64), axis, -1)
    blocks = v.reshape(v.shape[:-1] + (-1, 32))
    amax = np.abs(blocks).max(-1, keepdims=True)
    byte = np.maximum(np.where(amax > 0, np.frexp(amax)[1] - 1 + 127, 0) - down, 1)
    scale = np.exp2(byte - 127.0)
    codes = (blocks / scale).astype(np.float32).astype(dtype).astype(np.float64)
    return np.moveaxis((codes * scale).reshape(v.shape), -1, axis)


WIDE = False


def mx_kscale(k):
    if not WIDE:
        return np.ones(k)
    levels = np.array([10, -10, 5, -5, 0])
    if k % 512:
        return np.exp2(np.random.permutation(np.resize(levels, k // 32))).repeat(32)
    a = np.empty((k // 512, 16))
    for p in range(k // 512):
        a[p, :8] = np.random.permutation(np.resize(levels, 8))
        for g in range(8):
            far = levels[np.abs(levels - a[p, g]) >= 10]
            a[p, g + 8] = far[np.random.randint(len(far))]
    return np.exp2(a.ravel()).repeat(32)


def f64(x):
    return np.asarray(x).astype(np.float64)


def striped(idx):
    return np.tile(idx.reshape(-1, 16).T, (8, 1)).astype(np.uint16)


def unstriped(offs):
    return offs[:16].T.reshape(-1).astype(np.int64)


E2M1 = np.array([0.0, 0.5, 1.0, 1.5, 2.0, 3.0, 4.0, 6.0, -0.0, -0.5, -1.0, -1.5, -2.0, -3.0, -4.0, -6.0])


def pack_weight(w, fmt):
    k, n = w.shape
    w = f64(np.asarray(w, np.float32).astype(ml_dtypes.bfloat16)).reshape(k // 32, 32, n)
    amax = np.abs(w).max(1)
    if fmt == "e4m3":
        byte = np.frexp(amax)[1] - 1 + 127 - 7
    else:
        mant, ex = np.frexp(amax / 6.0)
        byte = np.where(mant > 0.5, ex, ex - 1) + 127
    byte = np.clip(np.where(amax > 0, byte, 1), 1, 254)
    scaled = (w * np.exp2(127.0 - byte)[:, None, :]).reshape(k, n).astype(np.float32)
    by_word = np.ascontiguousarray(scaled.reshape(k // 512, 128, 4, n).transpose(0, 1, 3, 2))
    if fmt == "e4m3":
        words = by_word.astype(ml_dtypes.float8_e4m3fn).view(np.uint8)
    else:
        c = by_word.astype(ml_dtypes.float4_e2m1fn).view(np.uint8) & 0xF
        words = (c[..., 0::2] | (c[..., 1::2] << 4)).reshape(k // 512, 128, 2 * n)
    return np.ascontiguousarray(words), np.ascontiguousarray(byte.astype(np.uint8).reshape(k // 512, 16, n))


def unpack_weight(words, scales, fmt):
    g, _, n = scales.shape
    words = np.ascontiguousarray(words).reshape(g, 128, n, -1)
    if fmt == "e4m3":
        vals = words.view(ml_dtypes.float8_e4m3fn).astype(np.float64)
    else:
        nib = np.empty((g, 128, n, 4), np.uint8)
        nib[..., 0::2] = words & 0xF
        nib[..., 1::2] = words >> 4
        vals = E2M1[nib]
    vals = vals * np.repeat(np.exp2(scales.astype(np.float64) - 127.0), 8, axis=1)[..., None]
    return vals.transpose(0, 1, 3, 2).reshape(g * 512, n)


def gelu(v):
    return 0.5 * v * (1.0 + np.tanh(np.sqrt(2.0 / np.pi) * (v + 0.044715 * v**3)))


K, T, S, H, T2, S2 = 1536, 2048, 1024, 512, 4096, 1024

def setup_inputs():
    n = np.random.standard_normal
    s = mx_kscale(K)[:, None]
    u = mx_kscale(H)[:, None]
    tab_words, tab_scales = pack_weight(n((K, T)) * s, "e4m3")
    tab2_words, tab2_scales = pack_weight(2.0 * n((H, T2)) / np.sqrt(H) / u, "e4m3")
    w1 = (n((K, H)) / np.sqrt(K) / s * u.T).astype(np.float32)
    w4_words, w4_scales = pack_weight(1.5 * n((K, H)) / np.sqrt(K) / s, "e2m1")
    cost = (0.4 * np.exp(0.3 * n(S2))).astype(np.float32)
    offs = striped(np.random.permutation(T)[:S])
    offs2 = striped(np.random.permutation(T2)[:S2])
    return {"tab_words": tab_words, "tab_scales": tab_scales, "offs": offs,
            "tab2_words": tab2_words, "tab2_scales": tab2_scales, "offs2": offs2,
            "w1": w1, "w4_words": w4_words, "w4_scales": w4_scales, "cost": cost}

def reference(tab_words, tab_scales, offs, tab2_words, tab2_scales, offs2, w1, w4_words, w4_scales, cost):
    v = unpack_weight(tab_words, tab_scales, "e4m3")[:, unstriped(offs)]
    v2 = unpack_weight(tab2_words, tab2_scales, "e4m3")[:, unstriped(offs2)]
    w1q = mxq(f64(w1), 0, "e4m3")
    w4 = unpack_weight(w4_words, w4_scales, "e2m1")
    a = w1q.T @ v
    b = w4.T @ v
    h = a * (1.0 / (1.0 + np.exp(-b)))
    hq = mxq(h, 0, "e4m3")
    z = v2.T @ hq
    return np.maximum(np.abs(z) - f64(cost)[:, None], 0.0)

@@ -1,0 +1,266 @@
+from contextlib import ExitStack
+
+import concourse.mybir as mybir
+from concourse.masks import make_identity
+
+K, T, S, H, T2, S2 = 1536, 2048, 1024, 512, 4096, 1024
+FLOPS = 2 * (2 * K * H * S + H * S2 * S)
+
+F32 = mybir.dt.float32
+BF16 = mybir.dt.bfloat16
+I32 = mybir.dt.int32
+U32 = mybir.dt.uint32
+U16 = mybir.dt.uint16
+U8 = mybir.dt.uint8
+FP8X4 = mybir.dt.float8_e4m3fn_x4
+FP4X4 = mybir.dt.float4_e2m1fn_x4
+ACT = mybir.ActivationFunctionType
+ALU = mybir.AluOpType
+
+P = 128
+PASSES = K // 512
+HALF = 512
+SHIFT_ROWS = 112
+
+
+def tile_list_pairs_tradable_edge_kernel(
+    tc, tab_words, tab_scales, offs, tab2_words, tab2_scales, offs2, w1, w4_words, w4_scales, cost, out
+):
+    nc = tc.nc
+    with ExitStack() as ctx:
+        keep = ctx.enter_context(tc.tile_pool(name="keep", bufs=1))
+        big = ctx.enter_context(tc.tile_pool(name="big", bufs=1))
+        work = ctx.enter_context(tc.tile_pool(name="work", bufs=4))
+        psum = ctx.enter_context(tc.psum_pool(name="psum", bufs=1))
+
+        def bank(n, shape, name):
+            return psum.tile(shape, F32, tag="bank%d" % n, name=name)
+
+        idx = keep.tile([P, S // 16], U16, name="idx")
+        idx2 = keep.tile([P, S2 // 16], U16, name="idx2")
+        nc.sync.dma_start(idx[:], offs)
+
+        KB = 1024
+        cost_rows = big.tile([P, 18 * P], F32, name="cost_rows", offset=32 * KB - 256, align_bytes=64)
+        tab_sc = big.tile([P, T // 4], I32, name="tab_sc", offset=48 * KB, align_bytes=64)
+        w4_sc = keep.tile([P, PASSES * H // 4], I32, name="w4_sc", align_bytes=64)
+        tab2_sc = keep.tile([P, T2 // 4], I32, name="tab2_sc", align_bytes=64)
+        v_sc_moved = keep.tile([P, (PASSES - 1) * S // 4], I32, name="v_sc_moved", align_bytes=64)
+        nc.vector.memset(cost_rows[:, 0:P], 0.0)
+        for t in (tab_sc, w4_sc, tab2_sc, v_sc_moved):
+            nc.vector.memset(t[:], 0)
+
+        def load_table(src, width, name, offset):
+            t = big.tile([P, width], I32, name=name, offset=offset, align_bytes=64)
+            nc.sync.dma_start(t[:], src.rearrange("p t i -> p (t i)").bitcast(I32))
+            return t
+
+        def load_w1(a, offset):
+            t = big.tile([P, 4, H], F32, name="w1_raw%d" % a, offset=offset, align_bytes=64)
+            nc.sync.dma_start(t[:], w1[512 * a : 512 * (a + 1), :].rearrange("(p i) r -> p i r", i=4))
+            return t
+
+        tab = [load_table(tab_words[0], T, "tab0", 4 * KB)]
+        w4 = keep.tile([P, PASSES, H // 2], I32, name="w4", align_bytes=64)
+        nc.sync.dma_start(w4[:], w4_words.bitcast(I32).rearrange("a p c -> p a c"))
+        nc.scalar.dma_start(cost_rows[0 : S2 // P, 0:P], cost.rearrange("(t p) -> t p", p=P))
+        for q in range(4):
+            nc.scalar.dma_start(tab_sc[32 * q : 32 * q + 4 * PASSES, :], tab_scales[:, 4 * q : 4 * q + 4, :].bitcast(I32))
+        for q in range(4):
+            nc.scalar.dma_start(
+                w4_sc[32 * q : 32 * q + 4, :].rearrange("p (a c) -> p a c", a=PASSES),
+                w4_scales[:, 4 * q : 4 * q + 4, :].bitcast(I32).rearrange("a r c -> r a c"),
+            )
+        ident = keep.tile([P, P], F32, name="ident")
+        make_identity(nc, ident[:])
+        cost_ps = bank(7, [P, P], "cost_ps")
+        nc.tensor.transpose(cost_ps[:], cost_rows[:, 0:P], ident[:])
+        cost_col = keep.tile([P, S2 // P], F32, name="cost_col")
+        nc.vector.tensor_copy(cost_col[:], cost_ps[:, 0 : S2 // P])
+        for q in range(4):
+            nc.gpsimd.dma_start(tab2_sc[32 * q : 32 * q + 4, :], tab2_scales[0, 4 * q : 4 * q + 4, :].bitcast(I32))
+        tab.append(load_table(tab_words[1], T, "tab1", 24 * KB))
+        w1_raw = [load_w1(0, 32 * KB)]
+        tab.append(load_table(tab_words[2], T, "tab2p", 40 * KB))
+        nc.sync.dma_start(idx2[:], offs2)
+
+        v = [keep.tile([P, S], U32, name="v%d" % a, align_bytes=64) for a in range(PASSES)]
+        v_sc = keep.tile([P, S], U8, name="v_sc", align_bytes=64)
+        v2 = keep.tile([P, S2], U32, name="v2", align_bytes=64)
+        v2_sc = keep.tile([P, S2], U8, name="v2_sc", align_bytes=64)
+
+        def gather(dst, window, lst, dt, lo, n):
+            nc.vector.tensor_copy(dst[:, lo : lo + n], window[:].bitcast(dt).indirect(lst[:, lo // 16 : (lo + n) // 16]))
+
+        def gather_scales():
+            gather(v_sc, tab_sc, idx, U8, 0, S)
+            for a in range(1, PASSES):
+                w0 = (a - 1) * S // 4
+                nc.scalar.dma_start(
+                    v_sc_moved[0:SHIFT_ROWS, w0 : w0 + S // 4],
+                    v_sc[4 * a : 4 * a + SHIFT_ROWS, :].bitcast(I32),
+                )
+
+        def v_scale(a, jt):
+            if a == 0:
+                return v_sc[:, P * jt : P * (jt + 1)]
+            c0 = (a - 1) * S + P * jt
+            return v_sc_moved[:].bitcast(U8)[:, c0 : c0 + P]
+
+        b_ps = [bank(jt, [P, H], "b%d" % jt) for jt in range(8)]
+        sig = [keep.tile([P, H], F32, name="sig%d" % jt) for jt in range(8)]
+
+        def permuted(ps):
+            return ps[:].rearrange("p (q u e) -> p u q e", u=2, e=2)
+
+        def b_pass(a, jts):
+            for jt in jts:
+                nc.tensor.matmul_mx(
+                    b_ps[jt][:],
+                    lhsT=v[a][:, P * jt : P * (jt + 1)].bitcast(FP8X4),
+                    lhsT_scale=v_scale(a, jt),
+                    rhs=w4[:, a, :].bitcast(U8).bitcast(FP4X4),
+                    rhs_scale=w4_sc[:].bitcast(U8)[:, H * a : H * (a + 1)],
+                    start=(a == 0),
+                    stop=(a == PASSES - 1),
+                )
+
+        def sigmoid(jts):
+            for jt in jts:
+                nc.scalar.activation(sig[jt][:].rearrange("p (u q e) -> p u q e", u=2, e=2), permuted(b_ps[jt]), ACT.Sigmoid)
+
+        w1_grp = [keep.tile([P, H, 4], BF16, name="w1_grp%d" % a, align_bytes=64) for a in range(PASSES)]
+        w1_q = keep.tile([P, PASSES, H], U32, name="w1_q", align_bytes=64)
+        w1_sc = keep.tile([P, PASSES, H], U8, name="w1_sc", align_bytes=64)
+
+        def interleave(a, c0, c1, copy):
+            copy(
+                w1_grp[a][:, c0:c1, :].rearrange("p (c m) i -> p c i m", m=4),
+                w1_raw[a][:, :, c0:c1].rearrange("p i (c m) -> p c i m", m=4),
+            )
+
+        def quantize_w1(a):
+            nc.vector.quantize_mx(w1_q[:, a, :].bitcast(FP8X4), w1_sc[:, a, :], w1_grp[a][:].rearrange("p c i -> p (c i)"))
+
+        a_ps = [bank(jt, [P, H], "a%d" % jt) for jt in range(8)]
+
+        def a_pass(a, jts):
+            for jt in jts:
+                nc.tensor.matmul_mx(
+                    a_ps[jt][:],
+                    lhsT=v[a][:, P * jt : P * (jt + 1)].bitcast(FP8X4),
+                    lhsT_scale=v_scale(a, jt),
+                    rhs=w1_q[:, a, :].bitcast(FP8X4),
+                    rhs_scale=w1_sc[:, a, :],
+                    start=(a == 0),
+                    stop=(a == PASSES - 1),
+                )
+
+        lo_j, hi_j = range(0, 4), range(4, 8)
+        gather(v[0], tab[0], idx, U32, 0, HALF)
+        gather_scales()
+        b_pass(0, lo_j)
+        gather(v[0], tab[0], idx, U32, HALF, HALF)
+        w1_raw.append(load_w1(1, 0))
+        w1_raw.append(load_w1(2, 8 * KB))
+        b_pass(0, hi_j)
+        gather(v[1], tab[1], idx, U32, 0, HALF)
+        b_pass(1, lo_j)
+        gather(v[1], tab[1], idx, U32, HALF, HALF)
+        tab2 = load_table(tab2_words[0], T2, "tab2", 16 * KB)
+        b_pass(1, hi_j)
+        interleave(0, 0, H, nc.scalar.copy)
+        gather(v[2], tab[2], idx, U32, 0, HALF // 2)
+        b_pass(2, range(0, 2))
+        gather(v[2], tab[2], idx, U32, HALF // 2, HALF // 2)
+        b_pass(2, range(2, 4))
+        sigmoid(lo_j)
+        quantize_w1(0)
+        gather(v[2], tab[2], idx, U32, HALF, HALF)
+        b_pass(2, hi_j)
+        a_pass(0, lo_j)
+        interleave(1, 0, 256, nc.vector.tensor_copy)
+        interleave(1, 256, H, nc.scalar.copy)
+        interleave(2, 0, 320, nc.vector.tensor_copy)
+        interleave(2, 320, H, nc.scalar.copy)
+        quantize_w1(1)
+        a_pass(1, lo_j)
+        quantize_w1(2)
+        a_pass(2, lo_j)
+        sigmoid(hi_j)
+        a_pass(0, hi_j)
+        a_pass(1, hi_j)
+
+        h_grp = keep.tile([P, S, 4], BF16, name="h_grp", align_bytes=64)
+        h_q = keep.tile([P, S], U32, name="h_q", align_bytes=64)
+        h_sc = keep.tile([P, S], U8, name="h_sc", align_bytes=64)
+
+        def gate(pair):
+            h_t = []
+            for jt in (2 * pair, 2 * pair + 1):
+                t = work.tile([P, H], BF16, tag="h_t", name="h_t%d" % jt)
+                nc.vector.tensor_tensor(
+                    t[:].rearrange("p (u q e) -> p u q e", u=2, e=2),
+                    permuted(a_ps[jt]),
+                    sig[jt][:].rearrange("p (u q e) -> p u q e", u=2, e=2),
+                    ALU.mult,
+                )
+                h_t.append(t)
+            ps = bank(2 * pair, [P, 2, 2, P], "h_ps%d" % pair)
+            for n in range(2):
+                for u in range(2):
+                    nc.tensor.transpose(ps[:, n, u, :], h_t[n][:].bitcast(F32)[:, P * u : P * (u + 1)], ident[:])
+            cols = slice(2 * P * pair, 2 * P * (pair + 1))
+            nc.scalar.copy(
+                h_grp[:, cols, :].rearrange("p j t -> p (j t)").bitcast(F32).rearrange("p (n j u) -> p n j u", n=2, u=2),
+                ps[:].rearrange("p n u j -> p n j u"),
+            )
+
+        def quantize_h(pair):
+            cols = slice(2 * P * pair, 2 * P * (pair + 1))
+            nc.vector.quantize_mx(h_q[:, cols].bitcast(FP8X4), h_sc[:, cols], h_grp[:, cols, :].rearrange("p j t -> p (j t)"))
+
+        def edge(it, half, bk, res):
+            cols = slice(HALF * half, HALF * (half + 1))
+            z = bank(bk, [P, HALF], "z%d_%d" % (it, half))
+            nc.tensor.matmul_mx(
+                z[:],
+                lhsT=v2[:, P * it : P * (it + 1)].bitcast(FP8X4),
+                lhsT_scale=v2_sc[:, P * it : P * (it + 1)],
+                rhs=h_q[:, cols].bitcast(FP8X4),
+                rhs_scale=h_sc[:, cols],
+                start=True,
+                stop=True,
+            )
+            mag = work.tile([P, HALF], F32, tag="mag", name="mag%d_%d" % (it, half))
+            nc.scalar.activation(mag[:], z[:], ACT.Abs)
+            nc.vector.tensor_scalar(res, mag[:], cost_col[:, it : it + 1], 0.0, ALU.subtract, ALU.max)
+
+        res = [keep.tile([P, S], F32, name="res%d" % it) for it in range(8)]
+
+        def edge_half(it, half, bk):
+            cols = slice(HALF * half, HALF * (half + 1))
+            edge(it, half, bk, res[it][:, cols])
+            nc.sync.dma_start(out[P * it : P * (it + 1), cols], res[it][:, cols])
+
+        gather(v2_sc, tab2_sc, idx2, U8, 0, HALF)
+        gate(0)
+        gate(1)
+        a_pass(2, hi_j)
+        quantize_h(0)
+        quantize_h(1)
+        gather(v2, tab2, idx2, U32, 0, HALF)
+        for it in range(4):
+            edge_half(it, 0, (1, 3, 0, 2)[it])
+        gate(2)
+        gate(3)
+        quantize_h(2)
+        quantize_h(3)
+        for it in range(4):
+            edge_half(it, 1, (5, 7, 1, 3)[it])
+        gather(v2_sc, tab2_sc, idx2, U8, HALF, HALF)
+        gather(v2, tab2, idx2, U32, HALF, HALF)
+        for it in range(4, 8):
+            for half in range(2):
+                edge(it, half, (0, 2, 4, 6, 5, 7, 1, 3)[2 * (it - 4) + half], res[it][:, HALF * half : HALF * (half + 1)])
+            nc.sync.dma_start(out[P * it : P * (it + 1), :], res[it][:])

@@ -30,7 +30,7 @@ def tile_list_pairs_tradable_edge_kernel(
     with ExitStack() as ctx:
         keep = ctx.enter_context(tc.tile_pool(name="keep", bufs=1))
         big = ctx.enter_context(tc.tile_pool(name="big", bufs=1))
-        work = ctx.enter_context(tc.tile_pool(name="work", bufs=4))
+        work = ctx.enter_context(tc.tile_pool(name="work", bufs=8))
         psum = ctx.enter_context(tc.psum_pool(name="psum", bufs=1))
 
         def bank(n, shape, name):
@@ -41,48 +41,45 @@ def tile_list_pairs_tradable_edge_kernel(
         nc.sync.dma_start(idx[:], offs)
 
         KB = 1024
-        cost_rows = big.tile([P, 18 * P], F32, name="cost_rows", offset=32 * KB - 256, align_bytes=64)
-        tab_sc = big.tile([P, T // 4], I32, name="tab_sc", offset=48 * KB, align_bytes=64)
+        tab_sc = keep.tile([P, T // 4], I32, name="tab_sc", align_bytes=64)
         w4_sc = keep.tile([P, PASSES * H // 4], I32, name="w4_sc", align_bytes=64)
         tab2_sc = keep.tile([P, T2 // 4], I32, name="tab2_sc", align_bytes=64)
         v_sc_moved = keep.tile([P, (PASSES - 1) * S // 4], I32, name="v_sc_moved", align_bytes=64)
-        nc.vector.memset(cost_rows[:, 0:P], 0.0)
-        for t in (tab_sc, w4_sc, tab2_sc, v_sc_moved):
+        cost_rows = keep.tile([P, P], F32, name="cost_rows")
+        nc.gpsimd.memset(tab_sc[:], 0)
+        for t in (w4_sc, tab2_sc, v_sc_moved):
             nc.vector.memset(t[:], 0)
-
-        def load_table(src, width, name, offset):
-            t = big.tile([P, width], I32, name=name, offset=offset, align_bytes=64)
-            nc.sync.dma_start(t[:], src.rearrange("p t i -> p (t i)").bitcast(I32))
-            return t
+        nc.vector.memset(cost_rows[:], 0.0)
+        ident = keep.tile([P, P], F32, name="ident")
+        nc.vector.memset(ident[:], 0.0)
 
         def load_w1(a, offset):
             t = big.tile([P, 4, H], F32, name="w1_raw%d" % a, offset=offset, align_bytes=64)
             nc.sync.dma_start(t[:], w1[512 * a : 512 * (a + 1), :].rearrange("(p i) r -> p i r", i=4))
             return t
 
-        tab = [load_table(tab_words[0], T, "tab0", 4 * KB)]
+        def load_table(src, width, name, offset):
+            t = big.tile([P, width], I32, name=name, offset=offset, align_bytes=64)
+            nc.sync.dma_start(t[:], src.rearrange("p t i -> p (t i)").bitcast(I32))
+            return t[:]
+
+        tab = [load_table(tab_words[0], T, "tab_0", 0)]
         w4 = keep.tile([P, PASSES, H // 2], I32, name="w4", align_bytes=64)
         nc.sync.dma_start(w4[:], w4_words.bitcast(I32).rearrange("a p c -> p a c"))
-        nc.scalar.dma_start(cost_rows[0 : S2 // P, 0:P], cost.rearrange("(t p) -> t p", p=P))
+        nc.sync.dma_start(idx2[:], offs2)
+        tab.append(load_table(tab_words[1], T, "tab_1", 36 * KB))
+        w1_raw = [load_w1(0, 8 * KB)]
+        tab.append(load_table(tab_words[2], T, "tab_2", 16 * KB))
         for q in range(4):
             nc.scalar.dma_start(tab_sc[32 * q : 32 * q + 4 * PASSES, :], tab_scales[:, 4 * q : 4 * q + 4, :].bitcast(I32))
-        for q in range(4):
+        for r in range(4):
             nc.scalar.dma_start(
-                w4_sc[32 * q : 32 * q + 4, :].rearrange("p (a c) -> p a c", a=PASSES),
-                w4_scales[:, 4 * q : 4 * q + 4, :].bitcast(I32).rearrange("a r c -> r a c"),
+                w4_sc[r:P:32, :].rearrange("p (a c) -> p a c", a=PASSES),
+                w4_scales[:, r:16:4, :].bitcast(I32).rearrange("a q c -> q a c"),
             )
-        ident = keep.tile([P, P], F32, name="ident")
-        make_identity(nc, ident[:])
-        cost_ps = bank(7, [P, P], "cost_ps")
-        nc.tensor.transpose(cost_ps[:], cost_rows[:, 0:P], ident[:])
-        cost_col = keep.tile([P, S2 // P], F32, name="cost_col")
-        nc.vector.tensor_copy(cost_col[:], cost_ps[:, 0 : S2 // P])
-        for q in range(4):
-            nc.gpsimd.dma_start(tab2_sc[32 * q : 32 * q + 4, :], tab2_scales[0, 4 * q : 4 * q + 4, :].bitcast(I32))
-        tab.append(load_table(tab_words[1], T, "tab1", 24 * KB))
-        w1_raw = [load_w1(0, 32 * KB)]
-        tab.append(load_table(tab_words[2], T, "tab2p", 40 * KB))
-        nc.sync.dma_start(idx2[:], offs2)
+        make_identity(nc, ident[:], nomemset=True)
+        warm = keep.tile([P, 1], F32, name="warm")
+        nc.scalar.activation(warm[:], cost_rows[:, 0:1], ACT.Sigmoid)
 
         v = [keep.tile([P, S], U32, name="v%d" % a, align_bytes=64) for a in range(PASSES)]
         v_sc = keep.tile([P, S], U8, name="v_sc", align_bytes=64)
@@ -90,15 +87,15 @@ def tile_list_pairs_tradable_edge_kernel(
         v2_sc = keep.tile([P, S2], U8, name="v2_sc", align_bytes=64)
 
         def gather(dst, window, lst, dt, lo, n):
-            nc.vector.tensor_copy(dst[:, lo : lo + n], window[:].bitcast(dt).indirect(lst[:, lo // 16 : (lo + n) // 16]))
+            nc.vector.tensor_copy(dst[:, lo : lo + n], window.bitcast(dt).indirect(lst[:, lo // 16 : (lo + n) // 16]))
 
-        def gather_scales():
-            gather(v_sc, tab_sc, idx, U8, 0, S)
+        def gather_scales(lo):
+            gather(v_sc, tab_sc[:], idx, U8, lo, HALF)
             for a in range(1, PASSES):
-                w0 = (a - 1) * S // 4
+                w0 = ((a - 1) * S + lo) // 4
                 nc.scalar.dma_start(
-                    v_sc_moved[0:SHIFT_ROWS, w0 : w0 + S // 4],
-                    v_sc[4 * a : 4 * a + SHIFT_ROWS, :].bitcast(I32),
+                    v_sc_moved[0:SHIFT_ROWS, w0 : w0 + HALF // 4],
+                    v_sc[4 * a : 4 * a + SHIFT_ROWS, lo : lo + HALF].bitcast(I32),
                 )
 
         def v_scale(a, jt):
@@ -158,29 +155,31 @@ def tile_list_pairs_tradable_edge_kernel(
 
         lo_j, hi_j = range(0, 4), range(4, 8)
         gather(v[0], tab[0], idx, U32, 0, HALF)
-        gather_scales()
+        gather_scales(0)
+        gather_scales(HALF)
+        for r in range(4):
+            nc.scalar.dma_start(tab2_sc[r:P:32, :], tab2_scales[0, r:16:4, :].bitcast(I32))
+        nc.scalar.dma_start(cost_rows[0 : S2 // P, :], cost.rearrange("(t p) -> t p", p=P))
         b_pass(0, lo_j)
-        gather(v[0], tab[0], idx, U32, HALF, HALF)
-        w1_raw.append(load_w1(1, 0))
-        w1_raw.append(load_w1(2, 8 * KB))
-        b_pass(0, hi_j)
         gather(v[1], tab[1], idx, U32, 0, HALF)
         b_pass(1, lo_j)
-        gather(v[1], tab[1], idx, U32, HALF, HALF)
-        tab2 = load_table(tab2_words[0], T2, "tab2", 16 * KB)
-        b_pass(1, hi_j)
+        gather(v[0], tab[0], idx, U32, HALF, HALF)
+        b_pass(0, hi_j)
         interleave(0, 0, H, nc.scalar.copy)
-        gather(v[2], tab[2], idx, U32, 0, HALF // 2)
-        b_pass(2, range(0, 2))
-        gather(v[2], tab[2], idx, U32, HALF // 2, HALF // 2)
-        b_pass(2, range(2, 4))
+        gather(v[1], tab[1], idx, U32, HALF, HALF)
+        w1_raw.append(load_w1(1, 32 * KB))
+        w1_raw.append(load_w1(2, 40 * KB))
+        gather(v[2], tab[2], idx, U32, 0, HALF)
+        b_pass(2, lo_j)
+        b_pass(1, hi_j)
         sigmoid(lo_j)
-        quantize_w1(0)
         gather(v[2], tab[2], idx, U32, HALF, HALF)
+        tab2 = load_table(tab2_words[0], T2, "tab2", 16 * KB)
+        quantize_w1(0)
         b_pass(2, hi_j)
         a_pass(0, lo_j)
-        interleave(1, 0, 256, nc.vector.tensor_copy)
-        interleave(1, 256, H, nc.scalar.copy)
+        interleave(1, 0, 320, nc.vector.tensor_copy)
+        interleave(1, 320, H, nc.scalar.copy)
         interleave(2, 0, 320, nc.vector.tensor_copy)
         interleave(2, 320, H, nc.scalar.copy)
         quantize_w1(1)
@@ -236,6 +235,7 @@ def tile_list_pairs_tradable_edge_kernel(
             nc.scalar.activation(mag[:], z[:], ACT.Abs)
             nc.vector.tensor_scalar(res, mag[:], cost_col[:, it : it + 1], 0.0, ALU.subtract, ALU.max)
 
+        cost_col = keep.tile([P, S2 // P], F32, name="cost_col")
         res = [keep.tile([P, S], F32, name="res%d" % it) for it in range(8)]
 
         def edge_half(it, half, bk):
@@ -243,24 +243,25 @@ def tile_list_pairs_tradable_edge_kernel(
             edge(it, half, bk, res[it][:, cols])
             nc.sync.dma_start(out[P * it : P * (it + 1), cols], res[it][:, cols])
 
-        gather(v2_sc, tab2_sc, idx2, U8, 0, HALF)
+        gather(v2_sc, tab2_sc[:], idx2, U8, 0, HALF)
+        gather(v2_sc, tab2_sc[:], idx2, U8, HALF, HALF)
         gate(0)
+        cost_ps = bank(1, [P, P], "cost_ps")
+        nc.tensor.transpose(cost_ps[:], cost_rows[:], ident[:])
+        nc.scalar.copy(cost_col[:], cost_ps[:, 0 : S2 // P])
         gate(1)
         a_pass(2, hi_j)
         quantize_h(0)
         quantize_h(1)
         gather(v2, tab2, idx2, U32, 0, HALF)
+        gather(v2, tab2, idx2, U32, HALF, HALF)
         for it in range(4):
-            edge_half(it, 0, (1, 3, 0, 2)[it])
+            edge_half(it, 0, (3, 1, 0, 2)[it])
         gate(2)
         gate(3)
         quantize_h(2)
         quantize_h(3)
-        for it in range(4):
-            edge_half(it, 1, (5, 7, 1, 3)[it])
-        gather(v2_sc, tab2_sc, idx2, U8, HALF, HALF)
-        gather(v2, tab2, idx2, U32, HALF, HALF)
         for it in range(4, 8):
-            for half in range(2):
-                edge(it, half, (0, 2, 4, 6, 5, 7, 1, 3)[2 * (it - 4) + half], res[it][:, HALF * half : HALF * (half + 1)])
-            nc.sync.dma_start(out[P * it : P * (it + 1), :], res[it][:])
+            edge_half(it, 0, (3, 1, 0, 2)[it - 4])
+        for it in range(8):
+            edge_half(it, 1, (5, 7, 4, 6, 3, 1, 0, 2)[it])

@@ -47,7 +47,8 @@ def tile_list_pairs_tradable_edge_kernel(
         v_sc_moved = keep.tile([P, (PASSES - 1) * S // 4], I32, name="v_sc_moved", align_bytes=64)
         cost_rows = keep.tile([P, P], F32, name="cost_rows")
         nc.gpsimd.memset(tab_sc[:], 0)
-        for t in (w4_sc, tab2_sc, v_sc_moved):
+        v2_sc_moved = keep.tile([P, S2 // 4], I32, name="v2_sc_moved", align_bytes=64)
+        for t in (w4_sc, tab2_sc, v_sc_moved, v2_sc_moved):
             nc.vector.memset(t[:], 0)
         nc.vector.memset(cost_rows[:], 0.0)
         ident = keep.tile([P, P], F32, name="ident")
@@ -69,6 +70,7 @@ def tile_list_pairs_tradable_edge_kernel(
         nc.sync.dma_start(idx2[:], offs2)
         tab.append(load_table(tab_words[1], T, "tab_1", 36 * KB))
         w1_raw = [load_w1(0, 8 * KB)]
+        nc.sync.dma_start(tab2_sc[0:P:8, :], tab2_scales[0].bitcast(I32))
         tab.append(load_table(tab_words[2], T, "tab_2", 16 * KB))
         for q in range(4):
             nc.scalar.dma_start(tab_sc[32 * q : 32 * q + 4 * PASSES, :], tab_scales[:, 4 * q : 4 * q + 4, :].bitcast(I32))
@@ -80,6 +82,7 @@ def tile_list_pairs_tradable_edge_kernel(
         make_identity(nc, ident[:], nomemset=True)
         warm = keep.tile([P, 1], F32, name="warm")
         nc.scalar.activation(warm[:], cost_rows[:, 0:1], ACT.Sigmoid)
+        nc.sync.dma_start(cost_rows[0 : S2 // P, :], cost.rearrange("(t p) -> t p", p=P))
 
         v = [keep.tile([P, S], U32, name="v%d" % a, align_bytes=64) for a in range(PASSES)]
         v_sc = keep.tile([P, S], U8, name="v_sc", align_bytes=64)
@@ -157,9 +160,6 @@ def tile_list_pairs_tradable_edge_kernel(
         gather(v[0], tab[0], idx, U32, 0, HALF)
         gather_scales(0)
         gather_scales(HALF)
-        for r in range(4):
-            nc.scalar.dma_start(tab2_sc[r:P:32, :], tab2_scales[0, r:16:4, :].bitcast(I32))
-        nc.scalar.dma_start(cost_rows[0 : S2 // P, :], cost.rearrange("(t p) -> t p", p=P))
         b_pass(0, lo_j)
         gather(v[1], tab[1], idx, U32, 0, HALF)
         b_pass(1, lo_j)
@@ -174,7 +174,7 @@ def tile_list_pairs_tradable_edge_kernel(
         b_pass(1, hi_j)
         sigmoid(lo_j)
         gather(v[2], tab[2], idx, U32, HALF, HALF)
-        tab2 = load_table(tab2_words[0], T2, "tab2", 16 * KB)
+        tab2 = load_table(tab2_words[0], T2, "tab2", 48 * KB)
         quantize_w1(0)
         b_pass(2, hi_j)
         a_pass(0, lo_j)
@@ -225,7 +225,7 @@ def tile_list_pairs_tradable_edge_kernel(
             nc.tensor.matmul_mx(
                 z[:],
                 lhsT=v2[:, P * it : P * (it + 1)].bitcast(FP8X4),
-                lhsT_scale=v2_sc[:, P * it : P * (it + 1)],
+                lhsT_scale=v2_sc_moved[:].bitcast(U8)[:, P * it : P * (it + 1)],
                 rhs=h_q[:, cols].bitcast(FP8X4),
                 rhs_scale=h_sc[:, cols],
                 start=True,
@@ -245,6 +245,8 @@ def tile_list_pairs_tradable_edge_kernel(
 
         gather(v2_sc, tab2_sc[:], idx2, U8, 0, HALF)
         gather(v2_sc, tab2_sc[:], idx2, U8, HALF, HALF)
+        for r in range(4):
+            nc.sync.dma_start(v2_sc_moved[r:P:32, :], v2_sc[8 * r : P : 32, :].bitcast(I32))
         gate(0)
         cost_ps = bank(1, [P, P], "cost_ps")
         nc.tensor.transpose(cost_ps[:], cost_rows[:], ident[:])

@@ -38,21 +38,25 @@ def tile_list_pairs_tradable_edge_kernel(
 
         idx = keep.tile([P, S // 16], U16, name="idx")
         idx2 = keep.tile([P, S2 // 16], U16, name="idx2")
+        nc.sync.dma_start(idx2[:], offs2)
         nc.sync.dma_start(idx[:], offs)
 
         KB = 1024
-        tab_sc = keep.tile([P, T // 4], I32, name="tab_sc", align_bytes=64)
+        tab_sc = big.tile([P, T // 4], I32, name="tab_sc", offset=8 * KB, align_bytes=64)
         w4_sc = keep.tile([P, PASSES * H // 4], I32, name="w4_sc", align_bytes=64)
-        tab2_sc = keep.tile([P, T2 // 4], I32, name="tab2_sc", align_bytes=64)
+        tab2_sc = big.tile([P, T2 // 4], I32, name="tab2_sc", offset=44 * KB, align_bytes=64)
         v_sc_moved = keep.tile([P, (PASSES - 1) * S // 4], I32, name="v_sc_moved", align_bytes=64)
         cost_rows = keep.tile([P, P], F32, name="cost_rows")
-        nc.gpsimd.memset(tab_sc[:], 0)
-        v2_sc_moved = keep.tile([P, S2 // 4], I32, name="v2_sc_moved", align_bytes=64)
-        for t in (w4_sc, tab2_sc, v_sc_moved, v2_sc_moved):
-            nc.vector.memset(t[:], 0)
-        nc.vector.memset(cost_rows[:], 0.0)
         ident = keep.tile([P, P], F32, name="ident")
+        nc.gpsimd.memset(tab2_sc[:, 0:640], 0)
+        nc.vector.memset(tab2_sc[:, 640 : T2 // 4], 0)
+        nc.gpsimd.memset(tab_sc[:], 0)
+        nc.vector.memset(w4_sc[:], 0)
+        nc.vector.memset(cost_rows[:], 0.0)
         nc.vector.memset(ident[:], 0.0)
+        v2_sc_moved = keep.tile([P, S2 // 4], I32, name="v2_sc_moved", align_bytes=64)
+        nc.vector.memset(v_sc_moved[:], 0)
+        nc.vector.memset(v2_sc_moved[:], 0)
 
         def load_w1(a, offset):
             t = big.tile([P, 4, H], F32, name="w1_raw%d" % a, offset=offset, align_bytes=64)
@@ -64,41 +68,57 @@ def tile_list_pairs_tradable_edge_kernel(
             nc.sync.dma_start(t[:], src.rearrange("p t i -> p (t i)").bitcast(I32))
             return t[:]
 
-        tab = [load_table(tab_words[0], T, "tab_0", 0)]
+        def load_tab_sc(q, queue):
+            queue.dma_start(tab_sc[32 * q : 32 * q + 4 * PASSES, :], tab_scales[:, 4 * q : 4 * q + 4, :].bitcast(I32))
+
+        tab_0 = big.tile([P, T], I32, name="tab_0", offset=29 * KB, align_bytes=64)
+        tab_0_src = tab_words[0].rearrange("p t i -> p (t i)").bitcast(I32)
+        nc.sync.dma_start(tab_0[:, 0 : T // 2], tab_0_src[:, 0 : T // 2])
+        nc.sync.dma_start(tab2_sc[0:P:8, :], tab2_scales[0].bitcast(I32))
+        nc.sync.dma_start(tab_0[:, T // 2 : T], tab_0_src[:, T // 2 : T])
+        tab = [tab_0[:]]
+        load_tab_sc(0, nc.scalar)
+        load_tab_sc(1, nc.scalar)
+        load_tab_sc(2, nc.sync)
+        load_tab_sc(3, nc.sync)
         w4 = keep.tile([P, PASSES, H // 2], I32, name="w4", align_bytes=64)
         nc.sync.dma_start(w4[:], w4_words.bitcast(I32).rearrange("a p c -> p a c"))
-        nc.sync.dma_start(idx2[:], offs2)
-        tab.append(load_table(tab_words[1], T, "tab_1", 36 * KB))
-        w1_raw = [load_w1(0, 8 * KB)]
-        nc.sync.dma_start(tab2_sc[0:P:8, :], tab2_scales[0].bitcast(I32))
-        tab.append(load_table(tab_words[2], T, "tab_2", 16 * KB))
-        for q in range(4):
-            nc.scalar.dma_start(tab_sc[32 * q : 32 * q + 4 * PASSES, :], tab_scales[:, 4 * q : 4 * q + 4, :].bitcast(I32))
+        w1_raw = [load_w1(0, 80 * KB)]
+        tab.append(load_table(tab_words[1], T, "tab_1", 56 * KB))
         for r in range(4):
-            nc.scalar.dma_start(
+            nc.gpsimd.dma_start(
                 w4_sc[r:P:32, :].rearrange("p (a c) -> p a c", a=PASSES),
                 w4_scales[:, r:16:4, :].bitcast(I32).rearrange("a q c -> q a c"),
             )
         make_identity(nc, ident[:], nomemset=True)
         warm = keep.tile([P, 1], F32, name="warm")
         nc.scalar.activation(warm[:], cost_rows[:, 0:1], ACT.Sigmoid)
-        nc.sync.dma_start(cost_rows[0 : S2 // P, :], cost.rearrange("(t p) -> t p", p=P))
 
-        v = [keep.tile([P, S], U32, name="v%d" % a, align_bytes=64) for a in range(PASSES)]
+        v = {(2, u): keep.tile([P, HALF], U32, name="v2_%d" % u, align_bytes=64) for u in range(2)}
+        v0 = big.tile([P, S], U32, name="v0", offset=9 * KB, align_bytes=64)
+        v1 = keep.tile([P, S], U32, name="v1", align_bytes=64)
+        v[0, 0], v[0, 1] = v0[:, 0:HALF], v0[:, HALF:S]
+        v[1, 0], v[1, 1] = v1[:, 0:HALF], v1[:, HALF:S]
         v_sc = keep.tile([P, S], U8, name="v_sc", align_bytes=64)
-        v2 = keep.tile([P, S2], U32, name="v2", align_bytes=64)
+        cand = [keep.tile([P, HALF], U32, name="cand0", align_bytes=64), big.tile([P, HALF], U32, name="cand1", offset=92 * KB, align_bytes=64)]
         v2_sc = keep.tile([P, S2], U8, name="v2_sc", align_bytes=64)
 
         def gather(dst, window, lst, dt, lo, n):
             nc.vector.tensor_copy(dst[:, lo : lo + n], window.bitcast(dt).indirect(lst[:, lo // 16 : (lo + n) // 16]))
 
-        def gather_scales(lo):
-            gather(v_sc, tab_sc[:], idx, U8, lo, HALF)
+        def gather_words(a, u):
+            nc.vector.tensor_copy(v[a, u][:], tab[a].bitcast(U32).indirect(idx[:, 32 * u : 32 * (u + 1)]))
+
+        def v_words(a, jt):
+            return v[a, jt // 4][:, P * (jt % 4) : P * (jt % 4 + 1)].bitcast(FP8X4)
+
+        def gather_scales():
+            gather(v_sc, tab_sc[:], idx, U8, 0, S)
             for a in range(1, PASSES):
-                w0 = ((a - 1) * S + lo) // 4
+                w0 = (a - 1) * S // 4
                 nc.scalar.dma_start(
-                    v_sc_moved[0:SHIFT_ROWS, w0 : w0 + HALF // 4],
-                    v_sc[4 * a : 4 * a + SHIFT_ROWS, lo : lo + HALF].bitcast(I32),
+                    v_sc_moved[0:SHIFT_ROWS, w0 : w0 + S // 4],
+                    v_sc[4 * a : 4 * a + SHIFT_ROWS, :].bitcast(I32),
                 )
 
         def v_scale(a, jt):
@@ -108,7 +128,10 @@ def tile_list_pairs_tradable_edge_kernel(
             return v_sc_moved[:].bitcast(U8)[:, c0 : c0 + P]
 
         b_ps = [bank(jt, [P, H], "b%d" % jt) for jt in range(8)]
-        sig = [keep.tile([P, H], F32, name="sig%d" % jt) for jt in range(8)]
+        sig_lo = big.tile([P, 4, H], F32, name="sig_lo", offset=33 * KB, align_bytes=64)
+        sig = [sig_lo[:, n, :] for n in range(4)]
+        sig_hi = big.tile([P, 4, H], F32, name="sig_hi", offset=14 * KB, align_bytes=64)
+        sig.extend(sig_hi[:, n, :] for n in range(4))
 
         def permuted(ps):
             return ps[:].rearrange("p (q u e) -> p u q e", u=2, e=2)
@@ -117,7 +140,7 @@ def tile_list_pairs_tradable_edge_kernel(
             for jt in jts:
                 nc.tensor.matmul_mx(
                     b_ps[jt][:],
-                    lhsT=v[a][:, P * jt : P * (jt + 1)].bitcast(FP8X4),
+                    lhsT=v_words(a, jt),
                     lhsT_scale=v_scale(a, jt),
                     rhs=w4[:, a, :].bitcast(U8).bitcast(FP4X4),
                     rhs_scale=w4_sc[:].bitcast(U8)[:, H * a : H * (a + 1)],
@@ -130,7 +153,8 @@ def tile_list_pairs_tradable_edge_kernel(
                 nc.scalar.activation(sig[jt][:].rearrange("p (u q e) -> p u q e", u=2, e=2), permuted(b_ps[jt]), ACT.Sigmoid)
 
         w1_grp = [keep.tile([P, H, 4], BF16, name="w1_grp%d" % a, align_bytes=64) for a in range(PASSES)]
-        w1_q = keep.tile([P, PASSES, H], U32, name="w1_q", align_bytes=64)
+        w1_q = [big.tile([P, H], U32, name="w1_q0", offset=1 * KB, align_bytes=64)]
+        w1_q.extend(keep.tile([P, H], U32, name="w1_q%d" % a, align_bytes=64) for a in range(1, PASSES))
         w1_sc = keep.tile([P, PASSES, H], U8, name="w1_sc", align_bytes=64)
 
         def interleave(a, c0, c1, copy):
@@ -140,7 +164,7 @@ def tile_list_pairs_tradable_edge_kernel(
             )
 
         def quantize_w1(a):
-            nc.vector.quantize_mx(w1_q[:, a, :].bitcast(FP8X4), w1_sc[:, a, :], w1_grp[a][:].rearrange("p c i -> p (c i)"))
+            nc.vector.quantize_mx(w1_q[a][:].bitcast(FP8X4), w1_sc[:, a, :], w1_grp[a][:].rearrange("p c i -> p (c i)"))
 
         a_ps = [bank(jt, [P, H], "a%d" % jt) for jt in range(8)]
 
@@ -148,56 +172,55 @@ def tile_list_pairs_tradable_edge_kernel(
             for jt in jts:
                 nc.tensor.matmul_mx(
                     a_ps[jt][:],
-                    lhsT=v[a][:, P * jt : P * (jt + 1)].bitcast(FP8X4),
+                    lhsT=v_words(a, jt),
                     lhsT_scale=v_scale(a, jt),
-                    rhs=w1_q[:, a, :].bitcast(FP8X4),
+                    rhs=w1_q[a][:].bitcast(FP8X4),
                     rhs_scale=w1_sc[:, a, :],
                     start=(a == 0),
                     stop=(a == PASSES - 1),
                 )
 
         lo_j, hi_j = range(0, 4), range(4, 8)
-        gather(v[0], tab[0], idx, U32, 0, HALF)
-        gather_scales(0)
-        gather_scales(HALF)
+        gather(v2_sc, tab2_sc[:], idx2, U8, 0, S2)
+        gather_scales()
+        tab.append(load_table(tab_words[2], T, "tab_2", 1 * KB))
+        gather_words(0, 0)
         b_pass(0, lo_j)
-        gather(v[1], tab[1], idx, U32, 0, HALF)
-        b_pass(1, lo_j)
-        gather(v[0], tab[0], idx, U32, HALF, HALF)
+        gather_words(0, 1)
         b_pass(0, hi_j)
+        for r in range(4):
+            nc.gpsimd.dma_start(v2_sc_moved[r:P:32, :], v2_sc[8 * r : P : 32, :].bitcast(I32))
+        w1_raw.append(load_w1(1, 33 * KB))
+        w1_raw.append(load_w1(2, 14 * KB))
         interleave(0, 0, H, nc.scalar.copy)
-        gather(v[1], tab[1], idx, U32, HALF, HALF)
-        w1_raw.append(load_w1(1, 32 * KB))
-        w1_raw.append(load_w1(2, 40 * KB))
-        gather(v[2], tab[2], idx, U32, 0, HALF)
+        gather(v1, tab[1], idx, U32, 0, S)
+        tab2 = load_table(tab2_words[0], T2, "tab2", 56 * KB)
+        nc.sync.dma_start(cost_rows[0 : S2 // P, :], cost.rearrange("(t p) -> t p", p=P))
+        b_pass(1, lo_j)
+        interleave(1, 0, H, nc.scalar.copy)
+        gather_words(2, 0)
         b_pass(2, lo_j)
         b_pass(1, hi_j)
         sigmoid(lo_j)
-        gather(v[2], tab[2], idx, U32, HALF, HALF)
-        tab2 = load_table(tab2_words[0], T2, "tab2", 48 * KB)
-        quantize_w1(0)
+        gather_words(2, 1)
         b_pass(2, hi_j)
-        a_pass(0, lo_j)
-        interleave(1, 0, 320, nc.vector.tensor_copy)
-        interleave(1, 320, H, nc.scalar.copy)
-        interleave(2, 0, 320, nc.vector.tensor_copy)
-        interleave(2, 320, H, nc.scalar.copy)
+        quantize_w1(0)
         quantize_w1(1)
-        a_pass(1, lo_j)
+        for jt in lo_j:
+            a_pass(0, [jt])
+            a_pass(1, [jt])
+        interleave(2, 0, H, nc.vector.tensor_copy)
         quantize_w1(2)
         a_pass(2, lo_j)
-        sigmoid(hi_j)
-        a_pass(0, hi_j)
-        a_pass(1, hi_j)
 
-        h_grp = keep.tile([P, S, 4], BF16, name="h_grp", align_bytes=64)
+        h_grp = [big.tile([P, HALF, 4], BF16, name="h_grp%d" % u, offset=(92 + 4 * u) * KB, align_bytes=64) for u in range(2)]
         h_q = keep.tile([P, S], U32, name="h_q", align_bytes=64)
         h_sc = keep.tile([P, S], U8, name="h_sc", align_bytes=64)
 
         def gate(pair):
             h_t = []
             for jt in (2 * pair, 2 * pair + 1):
-                t = work.tile([P, H], BF16, tag="h_t", name="h_t%d" % jt)
+                t = big.tile([P, H], BF16, name="h_t%d" % jt, offset=(56 + jt if jt >= 4 else 88 + jt) * KB, align_bytes=64)
                 nc.vector.tensor_tensor(
                     t[:].rearrange("p (u q e) -> p u q e", u=2, e=2),
                     permuted(a_ps[jt]),
@@ -209,22 +232,22 @@ def tile_list_pairs_tradable_edge_kernel(
             for n in range(2):
                 for u in range(2):
                     nc.tensor.transpose(ps[:, n, u, :], h_t[n][:].bitcast(F32)[:, P * u : P * (u + 1)], ident[:])
-            cols = slice(2 * P * pair, 2 * P * (pair + 1))
+            cols = slice(2 * P * (pair % 2), 2 * P * (pair % 2 + 1))
             nc.scalar.copy(
-                h_grp[:, cols, :].rearrange("p j t -> p (j t)").bitcast(F32).rearrange("p (n j u) -> p n j u", n=2, u=2),
+                h_grp[pair // 2][:, cols, :].rearrange("p j t -> p (j t)").bitcast(F32).rearrange("p (n j u) -> p n j u", n=2, u=2),
                 ps[:].rearrange("p n u j -> p n j u"),
             )
 
-        def quantize_h(pair):
-            cols = slice(2 * P * pair, 2 * P * (pair + 1))
-            nc.vector.quantize_mx(h_q[:, cols].bitcast(FP8X4), h_sc[:, cols], h_grp[:, cols, :].rearrange("p j t -> p (j t)"))
+        def quantize_h(half):
+            cols = slice(HALF * half, HALF * (half + 1))
+            nc.vector.quantize_mx(h_q[:, cols].bitcast(FP8X4), h_sc[:, cols], h_grp[half][:].rearrange("p j t -> p (j t)"))
 
         def edge(it, half, bk, res):
             cols = slice(HALF * half, HALF * (half + 1))
             z = bank(bk, [P, HALF], "z%d_%d" % (it, half))
             nc.tensor.matmul_mx(
                 z[:],
-                lhsT=v2[:, P * it : P * (it + 1)].bitcast(FP8X4),
+                lhsT=cand[it // 4][:, P * (it % 4) : P * (it % 4 + 1)].bitcast(FP8X4),
                 lhsT_scale=v2_sc_moved[:].bitcast(U8)[:, P * it : P * (it + 1)],
                 rhs=h_q[:, cols].bitcast(FP8X4),
                 rhs_scale=h_sc[:, cols],
@@ -243,26 +266,23 @@ def tile_list_pairs_tradable_edge_kernel(
             edge(it, half, bk, res[it][:, cols])
             nc.sync.dma_start(out[P * it : P * (it + 1), cols], res[it][:, cols])
 
-        gather(v2_sc, tab2_sc[:], idx2, U8, 0, HALF)
-        gather(v2_sc, tab2_sc[:], idx2, U8, HALF, HALF)
-        for r in range(4):
-            nc.sync.dma_start(v2_sc_moved[r:P:32, :], v2_sc[8 * r : P : 32, :].bitcast(I32))
         gate(0)
+        gate(1)
         cost_ps = bank(1, [P, P], "cost_ps")
         nc.tensor.transpose(cost_ps[:], cost_rows[:], ident[:])
         nc.scalar.copy(cost_col[:], cost_ps[:, 0 : S2 // P])
-        gate(1)
-        a_pass(2, hi_j)
+        sigmoid(hi_j)
+        nc.vector.tensor_copy(cand[0][:], tab2.bitcast(U32).indirect(idx2[:, 0:32]))
         quantize_h(0)
-        quantize_h(1)
-        gather(v2, tab2, idx2, U32, 0, HALF)
-        gather(v2, tab2, idx2, U32, HALF, HALF)
+        nc.vector.tensor_copy(cand[1][:], tab2.bitcast(U32).indirect(idx2[:, 32:64]))
+        for jt in hi_j:
+            for a in range(PASSES):
+                a_pass(a, [jt])
         for it in range(4):
             edge_half(it, 0, (3, 1, 0, 2)[it])
         gate(2)
         gate(3)
-        quantize_h(2)
-        quantize_h(3)
+        quantize_h(1)
         for it in range(4, 8):
             edge_half(it, 0, (3, 1, 0, 2)[it - 4])
         for it in range(8):

@@ -44,7 +44,7 @@ def tile_list_pairs_tradable_edge_kernel(
         KB = 1024
         tab_sc = big.tile([P, T // 4], I32, name="tab_sc", offset=8 * KB, align_bytes=64)
         w4_sc = keep.tile([P, PASSES * H // 4], I32, name="w4_sc", align_bytes=64)
-        tab2_sc = big.tile([P, T2 // 4], I32, name="tab2_sc", offset=44 * KB, align_bytes=64)
+        tab2_sc = big.tile([P, T2 // 4], I32, name="tab2_sc", offset=40 * KB, align_bytes=64)
         v_sc_moved = keep.tile([P, (PASSES - 1) * S // 4], I32, name="v_sc_moved", align_bytes=64)
         cost_rows = keep.tile([P, P], F32, name="cost_rows")
         ident = keep.tile([P, P], F32, name="ident")
@@ -71,7 +71,7 @@ def tile_list_pairs_tradable_edge_kernel(
         def load_tab_sc(q, queue):
             queue.dma_start(tab_sc[32 * q : 32 * q + 4 * PASSES, :], tab_scales[:, 4 * q : 4 * q + 4, :].bitcast(I32))
 
-        tab_0 = big.tile([P, T], I32, name="tab_0", offset=29 * KB, align_bytes=64)
+        tab_0 = big.tile([P, T], I32, name="tab_0", offset=24 * KB, align_bytes=64)
         tab_0_src = tab_words[0].rearrange("p t i -> p (t i)").bitcast(I32)
         nc.sync.dma_start(tab_0[:, 0 : T // 2], tab_0_src[:, 0 : T // 2])
         nc.sync.dma_start(tab2_sc[0:P:8, :], tab2_scales[0].bitcast(I32))
@@ -84,24 +84,24 @@ def tile_list_pairs_tradable_edge_kernel(
         w4 = keep.tile([P, PASSES, H // 2], I32, name="w4", align_bytes=64)
         nc.sync.dma_start(w4[:], w4_words.bitcast(I32).rearrange("a p c -> p a c"))
         w1_raw = [load_w1(0, 80 * KB)]
-        tab.append(load_table(tab_words[1], T, "tab_1", 56 * KB))
         for r in range(4):
-            nc.gpsimd.dma_start(
+            (nc.gpsimd if r < 2 else nc.sync).dma_start(
                 w4_sc[r:P:32, :].rearrange("p (a c) -> p a c", a=PASSES),
                 w4_scales[:, r:16:4, :].bitcast(I32).rearrange("a q c -> q a c"),
             )
+        tab.append(load_table(tab_words[1], T, "tab_1", 56 * KB))
         make_identity(nc, ident[:], nomemset=True)
         warm = keep.tile([P, 1], F32, name="warm")
         nc.scalar.activation(warm[:], cost_rows[:, 0:1], ACT.Sigmoid)
 
         v = {(2, u): keep.tile([P, HALF], U32, name="v2_%d" % u, align_bytes=64) for u in range(2)}
-        v0 = big.tile([P, S], U32, name="v0", offset=9 * KB, align_bytes=64)
         v1 = keep.tile([P, S], U32, name="v1", align_bytes=64)
-        v[0, 0], v[0, 1] = v0[:, 0:HALF], v0[:, HALF:S]
+        v[0, 0] = keep.tile([P, HALF], U32, name="v0_0", align_bytes=64)
+        v[0, 1] = big.tile([P, HALF], U32, name="v0_1", offset=9 * KB, align_bytes=64)
         v[1, 0], v[1, 1] = v1[:, 0:HALF], v1[:, HALF:S]
         v_sc = keep.tile([P, S], U8, name="v_sc", align_bytes=64)
         cand = [keep.tile([P, HALF], U32, name="cand0", align_bytes=64), big.tile([P, HALF], U32, name="cand1", offset=92 * KB, align_bytes=64)]
-        v2_sc = keep.tile([P, S2], U8, name="v2_sc", align_bytes=64)
+        v2_sc = [keep.tile([P, HALF], U8, name="v2_sc0", align_bytes=64), big.tile([P, HALF], U8, name="v2_sc1", offset=24 * KB, align_bytes=64)]
 
         def gather(dst, window, lst, dt, lo, n):
             nc.vector.tensor_copy(dst[:, lo : lo + n], window.bitcast(dt).indirect(lst[:, lo // 16 : (lo + n) // 16]))
@@ -111,6 +111,11 @@ def tile_list_pairs_tradable_edge_kernel(
 
         def v_words(a, jt):
             return v[a, jt // 4][:, P * (jt % 4) : P * (jt % 4 + 1)].bitcast(FP8X4)
+
+        def gather_cand_scales(u):
+            nc.vector.tensor_copy(v2_sc[u][:], tab2_sc[:].bitcast(U8).indirect(idx2[:, 32 * u : 32 * (u + 1)]))
+            for r in range(4):
+                nc.gpsimd.dma_start(v2_sc_moved[r:P:32, P * u : P * (u + 1)], v2_sc[u][8 * r : P : 32, :].bitcast(I32))
 
         def gather_scales():
             gather(v_sc, tab_sc[:], idx, U8, 0, S)
@@ -128,7 +133,7 @@ def tile_list_pairs_tradable_edge_kernel(
             return v_sc_moved[:].bitcast(U8)[:, c0 : c0 + P]
 
         b_ps = [bank(jt, [P, H], "b%d" % jt) for jt in range(8)]
-        sig_lo = big.tile([P, 4, H], F32, name="sig_lo", offset=33 * KB, align_bytes=64)
+        sig_lo = big.tile([P, 4, H], F32, name="sig_lo", offset=35 * KB, align_bytes=64)
         sig = [sig_lo[:, n, :] for n in range(4)]
         sig_hi = big.tile([P, 4, H], F32, name="sig_hi", offset=14 * KB, align_bytes=64)
         sig.extend(sig_hi[:, n, :] for n in range(4))
@@ -153,7 +158,7 @@ def tile_list_pairs_tradable_edge_kernel(
                 nc.scalar.activation(sig[jt][:].rearrange("p (u q e) -> p u q e", u=2, e=2), permuted(b_ps[jt]), ACT.Sigmoid)
 
         w1_grp = [keep.tile([P, H, 4], BF16, name="w1_grp%d" % a, align_bytes=64) for a in range(PASSES)]
-        w1_q = [big.tile([P, H], U32, name="w1_q0", offset=1 * KB, align_bytes=64)]
+        w1_q = [big.tile([P, H], U32, name="w1_q0", offset=33 * KB, align_bytes=64)]
         w1_q.extend(keep.tile([P, H], U32, name="w1_q%d" % a, align_bytes=64) for a in range(1, PASSES))
         w1_sc = keep.tile([P, PASSES, H], U8, name="w1_sc", align_bytes=64)
 
@@ -181,15 +186,14 @@ def tile_list_pairs_tradable_edge_kernel(
                 )
 
         lo_j, hi_j = range(0, 4), range(4, 8)
-        gather(v2_sc, tab2_sc[:], idx2, U8, 0, S2)
+        gather_cand_scales(0)
+        gather_words(0, 0)
         gather_scales()
         tab.append(load_table(tab_words[2], T, "tab_2", 1 * KB))
-        gather_words(0, 0)
         b_pass(0, lo_j)
         gather_words(0, 1)
         b_pass(0, hi_j)
-        for r in range(4):
-            nc.gpsimd.dma_start(v2_sc_moved[r:P:32, :], v2_sc[8 * r : P : 32, :].bitcast(I32))
+        gather_cand_scales(1)
         w1_raw.append(load_w1(1, 33 * KB))
         w1_raw.append(load_w1(2, 14 * KB))
         interleave(0, 0, H, nc.scalar.copy)
@@ -197,13 +201,14 @@ def tile_list_pairs_tradable_edge_kernel(
         tab2 = load_table(tab2_words[0], T2, "tab2", 56 * KB)
         nc.sync.dma_start(cost_rows[0 : S2 // P, :], cost.rearrange("(t p) -> t p", p=P))
         b_pass(1, lo_j)
-        interleave(1, 0, H, nc.scalar.copy)
+        interleave(1, 0, H // 2, nc.scalar.copy)
         gather_words(2, 0)
         b_pass(2, lo_j)
         b_pass(1, hi_j)
         sigmoid(lo_j)
         gather_words(2, 1)
         b_pass(2, hi_j)
+        interleave(1, H // 2, H, nc.vector.tensor_copy)
         quantize_w1(0)
         quantize_w1(1)
         for jt in lo_j:

@@ -38,8 +38,6 @@ def tile_list_pairs_tradable_edge_kernel(
 
         idx = keep.tile([P, S // 16], U16, name="idx")
         idx2 = keep.tile([P, S2 // 16], U16, name="idx2")
-        nc.sync.dma_start(idx2[:], offs2)
-        nc.sync.dma_start(idx[:], offs)
 
         KB = 1024
         tab_sc = big.tile([P, T // 4], I32, name="tab_sc", offset=8 * KB, align_bytes=64)
@@ -73,7 +71,9 @@ def tile_list_pairs_tradable_edge_kernel(
 
         tab_0 = big.tile([P, T], I32, name="tab_0", offset=24 * KB, align_bytes=64)
         tab_0_src = tab_words[0].rearrange("p t i -> p (t i)").bitcast(I32)
+        nc.sync.dma_start(idx2[:], offs2)
         nc.sync.dma_start(tab_0[:, 0 : T // 2], tab_0_src[:, 0 : T // 2])
+        nc.sync.dma_start(idx[:], offs)
         nc.sync.dma_start(tab2_sc[0:P:8, :], tab2_scales[0].bitcast(I32))
         nc.sync.dma_start(tab_0[:, T // 2 : T], tab_0_src[:, T // 2 : T])
         tab = [tab_0[:]]
@@ -100,7 +100,7 @@ def tile_list_pairs_tradable_edge_kernel(
         v[0, 1] = big.tile([P, HALF], U32, name="v0_1", offset=9 * KB, align_bytes=64)
         v[1, 0], v[1, 1] = v1[:, 0:HALF], v1[:, HALF:S]
         v_sc = keep.tile([P, S], U8, name="v_sc", align_bytes=64)
-        cand = [keep.tile([P, HALF], U32, name="cand0", align_bytes=64), big.tile([P, HALF], U32, name="cand1", offset=92 * KB, align_bytes=64)]
+        cand = [keep.tile([P, HALF], U32, name="cand0", align_bytes=64), big.tile([P, HALF], U32, name="cand1", offset=100 * KB, align_bytes=64)]
         v2_sc = [keep.tile([P, HALF], U8, name="v2_sc0", align_bytes=64), big.tile([P, HALF], U8, name="v2_sc1", offset=24 * KB, align_bytes=64)]
 
         def gather(dst, window, lst, dt, lo, n):
@@ -225,7 +225,7 @@ def tile_list_pairs_tradable_edge_kernel(
         def gate(pair):
             h_t = []
             for jt in (2 * pair, 2 * pair + 1):
-                t = big.tile([P, H], BF16, name="h_t%d" % jt, offset=(56 + jt if jt >= 4 else 88 + jt) * KB, align_bytes=64)
+                t = big.tile([P, H], BF16, name="h_t%d" % jt, offset=(88 + jt) * KB, align_bytes=64)
                 nc.vector.tensor_tensor(
                     t[:].rearrange("p (u q e) -> p u q e", u=2, e=2),
                     permuted(a_ps[jt]),
@@ -259,7 +259,10 @@ def tile_list_pairs_tradable_edge_kernel(
                 start=True,
                 stop=True,
             )
-            mag = work.tile([P, HALF], F32, tag="mag", name="mag%d_%d" % (it, half))
+            if (it, half) == (0, 0):
+                mag = big.tile([P, HALF], F32, name="mag_first", offset=100 * KB, align_bytes=64)
+            else:
+                mag = work.tile([P, HALF], F32, tag="mag", name="mag%d_%d" % (it, half))
             nc.scalar.activation(mag[:], z[:], ACT.Abs)
             nc.vector.tensor_scalar(res, mag[:], cost_col[:, it : it + 1], 0.0, ALU.subtract, ALU.max)
 
@@ -279,11 +282,12 @@ def tile_list_pairs_tradable_edge_kernel(
         sigmoid(hi_j)
         nc.vector.tensor_copy(cand[0][:], tab2.bitcast(U32).indirect(idx2[:, 0:32]))
         quantize_h(0)
-        nc.vector.tensor_copy(cand[1][:], tab2.bitcast(U32).indirect(idx2[:, 32:64]))
         for jt in hi_j:
             for a in range(PASSES):
                 a_pass(a, [jt])
-        for it in range(4):
+        edge_half(0, 0, 3)
+        nc.vector.tensor_copy(cand[1][:], tab2.bitcast(U32).indirect(idx2[:, 32:64]))
+        for it in range(1, 4):
             edge_half(it, 0, (3, 1, 0, 2)[it])
         gate(2)
         gate(3)

@@ -42,7 +42,7 @@ def tile_list_pairs_tradable_edge_kernel(
         KB = 1024
         tab_sc = big.tile([P, T // 4], I32, name="tab_sc", offset=8 * KB, align_bytes=64)
         w4_sc = keep.tile([P, PASSES * H // 4], I32, name="w4_sc", align_bytes=64)
-        tab2_sc = big.tile([P, T2 // 4], I32, name="tab2_sc", offset=40 * KB, align_bytes=64)
+        tab2_sc = big.tile([P, T2 // 4], I32, name="tab2_sc", offset=44 * KB, align_bytes=64)
         v_sc_moved = keep.tile([P, (PASSES - 1) * S // 4], I32, name="v_sc_moved", align_bytes=64)
         cost_rows = keep.tile([P, P], F32, name="cost_rows")
         ident = keep.tile([P, P], F32, name="ident")
@@ -52,9 +52,7 @@ def tile_list_pairs_tradable_edge_kernel(
         nc.vector.memset(w4_sc[:], 0)
         nc.vector.memset(cost_rows[:], 0.0)
         nc.vector.memset(ident[:], 0.0)
-        v2_sc_moved = keep.tile([P, S2 // 4], I32, name="v2_sc_moved", align_bytes=64)
         nc.vector.memset(v_sc_moved[:], 0)
-        nc.vector.memset(v2_sc_moved[:], 0)
 
         def load_w1(a, offset):
             t = big.tile([P, 4, H], F32, name="w1_raw%d" % a, offset=offset, align_bytes=64)
@@ -69,7 +67,7 @@ def tile_list_pairs_tradable_edge_kernel(
         def load_tab_sc(q, queue):
             queue.dma_start(tab_sc[32 * q : 32 * q + 4 * PASSES, :], tab_scales[:, 4 * q : 4 * q + 4, :].bitcast(I32))
 
-        tab_0 = big.tile([P, T], I32, name="tab_0", offset=24 * KB, align_bytes=64)
+        tab_0 = big.tile([P, T], I32, name="tab_0", offset=29 * KB, align_bytes=64)
         tab_0_src = tab_words[0].rearrange("p t i -> p (t i)").bitcast(I32)
         nc.sync.dma_start(idx2[:], offs2)
         nc.sync.dma_start(tab_0[:, 0 : T // 2], tab_0_src[:, 0 : T // 2])
@@ -96,12 +94,12 @@ def tile_list_pairs_tradable_edge_kernel(
 
         v = {(2, u): keep.tile([P, HALF], U32, name="v2_%d" % u, align_bytes=64) for u in range(2)}
         v1 = keep.tile([P, S], U32, name="v1", align_bytes=64)
-        v[0, 0] = keep.tile([P, HALF], U32, name="v0_0", align_bytes=64)
-        v[0, 1] = big.tile([P, HALF], U32, name="v0_1", offset=9 * KB, align_bytes=64)
+        v0 = big.tile([P, S], U32, name="v0", offset=9 * KB, align_bytes=64)
+        v[0, 0], v[0, 1] = v0[:, 0:HALF], v0[:, HALF:S]
         v[1, 0], v[1, 1] = v1[:, 0:HALF], v1[:, HALF:S]
         v_sc = keep.tile([P, S], U8, name="v_sc", align_bytes=64)
         cand = [keep.tile([P, HALF], U32, name="cand0", align_bytes=64), big.tile([P, HALF], U32, name="cand1", offset=100 * KB, align_bytes=64)]
-        v2_sc = [keep.tile([P, HALF], U8, name="v2_sc0", align_bytes=64), big.tile([P, HALF], U8, name="v2_sc1", offset=24 * KB, align_bytes=64)]
+        v2_sc = keep.tile([P, S2], U8, name="v2_sc", align_bytes=64)
 
         def gather(dst, window, lst, dt, lo, n):
             nc.vector.tensor_copy(dst[:, lo : lo + n], window.bitcast(dt).indirect(lst[:, lo // 16 : (lo + n) // 16]))
@@ -111,11 +109,6 @@ def tile_list_pairs_tradable_edge_kernel(
 
         def v_words(a, jt):
             return v[a, jt // 4][:, P * (jt % 4) : P * (jt % 4 + 1)].bitcast(FP8X4)
-
-        def gather_cand_scales(u):
-            nc.vector.tensor_copy(v2_sc[u][:], tab2_sc[:].bitcast(U8).indirect(idx2[:, 32 * u : 32 * (u + 1)]))
-            for r in range(4):
-                nc.gpsimd.dma_start(v2_sc_moved[r:P:32, P * u : P * (u + 1)], v2_sc[u][8 * r : P : 32, :].bitcast(I32))
 
         def gather_scales():
             gather(v_sc, tab_sc[:], idx, U8, 0, S)
@@ -186,17 +179,20 @@ def tile_list_pairs_tradable_edge_kernel(
                 )
 
         lo_j, hi_j = range(0, 4), range(4, 8)
-        gather_cand_scales(0)
-        gather_words(0, 0)
+        gather(v2_sc, tab2_sc[:], idx2, U8, 0, S2)
         gather_scales()
         tab.append(load_table(tab_words[2], T, "tab_2", 1 * KB))
+        gather_words(0, 0)
         b_pass(0, lo_j)
         gather_words(0, 1)
         b_pass(0, hi_j)
-        gather_cand_scales(1)
         w1_raw.append(load_w1(1, 33 * KB))
         w1_raw.append(load_w1(2, 14 * KB))
         interleave(0, 0, H, nc.scalar.copy)
+        v2_sc_moved = big.tile([P, S2 // 4], I32, name="v2_sc_moved", offset=80 * KB, align_bytes=64)
+        nc.gpsimd.memset(v2_sc_moved[:], 0)
+        for r in range(4):
+            nc.scalar.dma_start(v2_sc_moved[r:P:32, :], v2_sc[8 * r : P : 32, :].bitcast(I32))
         gather(v1, tab[1], idx, U32, 0, S)
         tab2 = load_table(tab2_words[0], T2, "tab2", 56 * KB)
         nc.sync.dma_start(cost_rows[0 : S2 // P, :], cost.rearrange("(t p) -> t p", p=P))

@@ -46,9 +46,8 @@ def tile_list_pairs_tradable_edge_kernel(
         v_sc_moved = keep.tile([P, (PASSES - 1) * S // 4], I32, name="v_sc_moved", align_bytes=64)
         cost_rows = keep.tile([P, P], F32, name="cost_rows")
         ident = keep.tile([P, P], F32, name="ident")
-        nc.gpsimd.memset(tab2_sc[:, 0:640], 0)
-        nc.vector.memset(tab2_sc[:, 640 : T2 // 4], 0)
         nc.gpsimd.memset(tab_sc[:], 0)
+        nc.vector.memset(tab2_sc[:], 0)
         nc.vector.memset(w4_sc[:], 0)
         nc.vector.memset(cost_rows[:], 0.0)
         nc.vector.memset(ident[:], 0.0)
@@ -75,9 +74,9 @@ def tile_list_pairs_tradable_edge_kernel(
         nc.sync.dma_start(tab2_sc[0:P:8, :], tab2_scales[0].bitcast(I32))
         nc.sync.dma_start(tab_0[:, T // 2 : T], tab_0_src[:, T // 2 : T])
         tab = [tab_0[:]]
-        load_tab_sc(0, nc.scalar)
+        load_tab_sc(0, nc.gpsimd)
         load_tab_sc(1, nc.scalar)
-        load_tab_sc(2, nc.sync)
+        load_tab_sc(2, nc.scalar)
         load_tab_sc(3, nc.sync)
         w4 = keep.tile([P, PASSES, H // 2], I32, name="w4", align_bytes=64)
         nc.sync.dma_start(w4[:], w4_words.bitcast(I32).rearrange("a p c -> p a c"))
@@ -157,8 +156,8 @@ def tile_list_pairs_tradable_edge_kernel(
 
         def interleave(a, c0, c1, copy):
             copy(
-                w1_grp[a][:, c0:c1, :].rearrange("p (c m) i -> p c i m", m=4),
-                w1_raw[a][:, :, c0:c1].rearrange("p i (c m) -> p c i m", m=4),
+                w1_grp[a][:, c0:c1, :].rearrange("p (c m) i -> p c i m", m=2),
+                w1_raw[a][:, :, c0:c1].rearrange("p i (c m) -> p c i m", m=2),
             )
 
         def quantize_w1(a):

@@ -44,12 +44,12 @@ def tile_list_pairs_tradable_edge_kernel(
         w4_sc = keep.tile([P, PASSES * H // 4], I32, name="w4_sc", align_bytes=64)
         tab2_sc = big.tile([P, T2 // 4], I32, name="tab2_sc", offset=44 * KB, align_bytes=64)
         v_sc_moved = keep.tile([P, (PASSES - 1) * S // 4], I32, name="v_sc_moved", align_bytes=64)
-        cost_rows = keep.tile([P, P], F32, name="cost_rows")
+        warm_in = keep.tile([P, 1], F32, name="warm_in")
         ident = keep.tile([P, P], F32, name="ident")
         nc.gpsimd.memset(tab_sc[:], 0)
         nc.vector.memset(tab2_sc[:], 0)
         nc.vector.memset(w4_sc[:], 0)
-        nc.vector.memset(cost_rows[:], 0.0)
+        nc.vector.memset(warm_in[:], 0.0)
         nc.vector.memset(ident[:], 0.0)
         nc.vector.memset(v_sc_moved[:], 0)
 
@@ -89,7 +89,7 @@ def tile_list_pairs_tradable_edge_kernel(
         tab.append(load_table(tab_words[1], T, "tab_1", 56 * KB))
         make_identity(nc, ident[:], nomemset=True)
         warm = keep.tile([P, 1], F32, name="warm")
-        nc.scalar.activation(warm[:], cost_rows[:, 0:1], ACT.Sigmoid)
+        nc.scalar.activation(warm[:], warm_in[:], ACT.Sigmoid)
 
         v = {(2, u): keep.tile([P, HALF], U32, name="v2_%d" % u, align_bytes=64) for u in range(2)}
         v1 = keep.tile([P, S], U32, name="v1", align_bytes=64)
@@ -194,7 +194,7 @@ def tile_list_pairs_tradable_edge_kernel(
             nc.scalar.dma_start(v2_sc_moved[r:P:32, :], v2_sc[8 * r : P : 32, :].bitcast(I32))
         gather(v1, tab[1], idx, U32, 0, S)
         tab2 = load_table(tab2_words[0], T2, "tab2", 56 * KB)
-        nc.sync.dma_start(cost_rows[0 : S2 // P, :], cost.rearrange("(t p) -> t p", p=P))
+        cost_col = big.tile([P, S2 // P], F32, name="cost_col", offset=1 * KB)
         b_pass(1, lo_j)
         interleave(1, 0, H // 2, nc.scalar.copy)
         gather_words(2, 0)
@@ -202,6 +202,8 @@ def tile_list_pairs_tradable_edge_kernel(
         b_pass(1, hi_j)
         sigmoid(lo_j)
         gather_words(2, 1)
+        with nc.allow_non_contiguous_dma(reason="one cost a partition and candidate tile"):
+            nc.sync.dma_start(cost_col[:], cost.rearrange("(t p) -> p t", p=P))
         b_pass(2, hi_j)
         interleave(1, H // 2, H, nc.vector.tensor_copy)
         quantize_w1(0)
@@ -261,7 +263,6 @@ def tile_list_pairs_tradable_edge_kernel(
             nc.scalar.activation(mag[:], z[:], ACT.Abs)
             nc.vector.tensor_scalar(res, mag[:], cost_col[:, it : it + 1], 0.0, ALU.subtract, ALU.max)
 
-        cost_col = keep.tile([P, S2 // P], F32, name="cost_col")
         res = [keep.tile([P, S], F32, name="res%d" % it) for it in range(8)]
 
         def edge_half(it, half, bk):
@@ -271,9 +272,6 @@ def tile_list_pairs_tradable_edge_kernel(
 
         gate(0)
         gate(1)
-        cost_ps = bank(1, [P, P], "cost_ps")
-        nc.tensor.transpose(cost_ps[:], cost_rows[:], ident[:])
-        nc.scalar.copy(cost_col[:], cost_ps[:, 0 : S2 // P])
         sigmoid(hi_j)
         nc.vector.tensor_copy(cand[0][:], tab2.bitcast(U32).indirect(idx2[:, 0:32]))
         quantize_h(0)

@@ -156,8 +156,8 @@ def tile_list_pairs_tradable_edge_kernel(
 
         def interleave(a, c0, c1, copy):
             copy(
-                w1_grp[a][:, c0:c1, :].rearrange("p (c m) i -> p c i m", m=2),
-                w1_raw[a][:, :, c0:c1].rearrange("p i (c m) -> p c i m", m=2),
+                w1_grp[a][:, c0:c1, :].rearrange("p (c m) i -> p c i m", m=4),
+                w1_raw[a][:, :, c0:c1].rearrange("p i (c m) -> p c i m", m=4),
             )
 
         def quantize_w1(a):

@@ -20,7 +20,8 @@ ALU = mybir.AluOpType
 P = 128
 PASSES = K // 512
 HALF = 512
-SHIFT_ROWS = 112
+EARLY = 4
+KB = 1024
 
 
 def tile_list_pairs_tradable_edge_kernel(
@@ -29,94 +30,80 @@ def tile_list_pairs_tradable_edge_kernel(
     nc = tc.nc
     with ExitStack() as ctx:
         keep = ctx.enter_context(tc.tile_pool(name="keep", bufs=1))
-        big = ctx.enter_context(tc.tile_pool(name="big", bufs=1))
+        shared = ctx.enter_context(tc.tile_pool(name="shared", bufs=1))
         work = ctx.enter_context(tc.tile_pool(name="work", bufs=8))
         psum = ctx.enter_context(tc.psum_pool(name="psum", bufs=1))
 
         def bank(n, shape, name):
             return psum.tile(shape, F32, tag="bank%d" % n, name=name)
 
+        def kept(shape, dt, name):
+            return keep.tile(shape, dt, name=name, align_bytes=64)
+
         idx = keep.tile([P, S // 16], U16, name="idx")
         idx2 = keep.tile([P, S2 // 16], U16, name="idx2")
 
-        KB = 1024
-        tab_sc = big.tile([P, T // 4], I32, name="tab_sc", offset=8 * KB, align_bytes=64)
-        w4_sc = keep.tile([P, PASSES * H // 4], I32, name="w4_sc", align_bytes=64)
-        tab2_sc = big.tile([P, T2 // 4], I32, name="tab2_sc", offset=44 * KB, align_bytes=64)
-        v_sc_moved = keep.tile([P, (PASSES - 1) * S // 4], I32, name="v_sc_moved", align_bytes=64)
-        warm_in = keep.tile([P, 1], F32, name="warm_in")
-        ident = keep.tile([P, P], F32, name="ident")
-        nc.gpsimd.memset(tab_sc[:], 0)
-        nc.vector.memset(tab2_sc[:], 0)
+        tab_sc = shared.tile([P, T // 4], I32, name="tab_sc", offset=0, align_bytes=64)
+        w4_sc = kept([P, PASSES * H // 4], I32, "w4_sc")
+        tab2_sc = kept([P, T2 // 4], I32, "tab2_sc")
+        v_sc_moved = kept([P, (PASSES - 1) * S // 4], I32, "v_sc_moved")
+        v2_sc_moved = kept([P, S2 // 4], I32, "v2_sc_moved")
+        ident = kept([P, P], F32, "ident")
+        nc.vector.memset(tab2_sc[:, 0 : T2 // 8], 0)
+        nc.gpsimd.memset(tab2_sc[:, T2 // 8 : T2 // 4], 0)
+        nc.vector.memset(tab_sc[:], 0)
         nc.vector.memset(w4_sc[:], 0)
-        nc.vector.memset(warm_in[:], 0.0)
-        nc.vector.memset(ident[:], 0.0)
         nc.vector.memset(v_sc_moved[:], 0)
+        nc.gpsimd.memset(v2_sc_moved[:], 0)
+        make_identity(nc, ident[:])
 
-        def load_w1(a, offset):
-            t = big.tile([P, 4, H], F32, name="w1_raw%d" % a, offset=offset, align_bytes=64)
+        def load_words(src, width, name):
+            t = kept([P, width], I32, name)
+            nc.sync.dma_start(t[:], src.rearrange("p t i -> p (t i)").bitcast(I32))
+            return t
+
+        def load_w1(a, t):
             nc.sync.dma_start(t[:], w1[512 * a : 512 * (a + 1), :].rearrange("(p i) r -> p i r", i=4))
             return t
 
-        def load_table(src, width, name, offset):
-            t = big.tile([P, width], I32, name=name, offset=offset, align_bytes=64)
-            nc.sync.dma_start(t[:], src.rearrange("p t i -> p (t i)").bitcast(I32))
-            return t[:]
-
-        def load_tab_sc(q, queue):
-            queue.dma_start(tab_sc[32 * q : 32 * q + 4 * PASSES, :], tab_scales[:, 4 * q : 4 * q + 4, :].bitcast(I32))
-
-        tab_0 = big.tile([P, T], I32, name="tab_0", offset=29 * KB, align_bytes=64)
+        tab_0 = kept([P, T], I32, "tab_0")
         tab_0_src = tab_words[0].rearrange("p t i -> p (t i)").bitcast(I32)
         nc.sync.dma_start(idx2[:], offs2)
-        nc.sync.dma_start(tab_0[:, 0 : T // 2], tab_0_src[:, 0 : T // 2])
         nc.sync.dma_start(idx[:], offs)
+        nc.sync.dma_start(tab_0[:, 0 : 3 * T // 8], tab_0_src[:, 0 : 3 * T // 8])
         nc.sync.dma_start(tab2_sc[0:P:8, :], tab2_scales[0].bitcast(I32))
-        nc.sync.dma_start(tab_0[:, T // 2 : T], tab_0_src[:, T // 2 : T])
-        tab = [tab_0[:]]
-        load_tab_sc(0, nc.gpsimd)
-        load_tab_sc(1, nc.scalar)
-        load_tab_sc(2, nc.scalar)
-        load_tab_sc(3, nc.sync)
-        w4 = keep.tile([P, PASSES, H // 2], I32, name="w4", align_bytes=64)
-        nc.sync.dma_start(w4[:], w4_words.bitcast(I32).rearrange("a p c -> p a c"))
-        w1_raw = [load_w1(0, 80 * KB)]
+        nc.sync.dma_start(tab_0[:, 3 * T // 8 : T], tab_0_src[:, 3 * T // 8 : T])
         for r in range(4):
-            (nc.gpsimd if r < 2 else nc.sync).dma_start(
+            nc.sync.dma_start(tab_sc[r:P:32, :], tab_scales[0, r:16:4, :].bitcast(I32))
+        for a in range(1, PASSES):
+            nc.sync.dma_start(tab_sc[3 + a : P : 8, :], tab_scales[a].bitcast(I32))
+        tab = [tab_0, load_words(tab_words[1], T, "tab_1")]
+        warm = keep.tile([P, 1], F32, name="warm")
+        nc.scalar.activation(warm[:], ident[:, 0:1], ACT.Sigmoid)
+        w4 = kept([P, PASSES, H // 2], I32, "w4")
+        nc.sync.dma_start(w4[:], w4_words.bitcast(I32).rearrange("a p c -> p a c"))
+        for r in range(4):
+            nc.sync.dma_start(
                 w4_sc[r:P:32, :].rearrange("p (a c) -> p a c", a=PASSES),
                 w4_scales[:, r:16:4, :].bitcast(I32).rearrange("a q c -> q a c"),
             )
-        tab.append(load_table(tab_words[1], T, "tab_1", 56 * KB))
-        make_identity(nc, ident[:], nomemset=True)
-        warm = keep.tile([P, 1], F32, name="warm")
-        nc.scalar.activation(warm[:], warm_in[:], ACT.Sigmoid)
+        tab.append(load_words(tab_words[2], T, "tab_2"))
 
-        v = {(2, u): keep.tile([P, HALF], U32, name="v2_%d" % u, align_bytes=64) for u in range(2)}
-        v1 = keep.tile([P, S], U32, name="v1", align_bytes=64)
-        v0 = big.tile([P, S], U32, name="v0", offset=9 * KB, align_bytes=64)
-        v[0, 0], v[0, 1] = v0[:, 0:HALF], v0[:, HALF:S]
-        v[1, 0], v[1, 1] = v1[:, 0:HALF], v1[:, HALF:S]
-        v_sc = keep.tile([P, S], U8, name="v_sc", align_bytes=64)
-        cand = [keep.tile([P, HALF], U32, name="cand0", align_bytes=64), big.tile([P, HALF], U32, name="cand1", offset=100 * KB, align_bytes=64)]
-        v2_sc = keep.tile([P, S2], U8, name="v2_sc", align_bytes=64)
+        v_sc = kept([P, S], U8, "v_sc")
+        v2_sc = kept([P, S2], U8, "v2_sc")
+        v = [shared.tile([P, S], U32, name="v0", offset=0, align_bytes=64), kept([P, S], U32, "v1"), kept([P, S], U32, "v2")]
+        cand = kept([P, S2], U32, "cand")
 
         def gather(dst, window, lst, dt, lo, n):
-            nc.vector.tensor_copy(dst[:, lo : lo + n], window.bitcast(dt).indirect(lst[:, lo // 16 : (lo + n) // 16]))
+            nc.vector.tensor_copy(dst[:, lo : lo + n], window[:].bitcast(dt).indirect(lst[:, lo // 16 : (lo + n) // 16]))
 
-        def gather_words(a, u):
-            nc.vector.tensor_copy(v[a, u][:], tab[a].bitcast(U32).indirect(idx[:, 32 * u : 32 * (u + 1)]))
+        def move_plane(a):
+            w0 = (a - 1) * S // 4
+            for r in range(4):
+                nc.sync.dma_start(v_sc_moved[r:P:32, w0 : w0 + S // 4], v_sc[8 * r + 3 + a : P : 32, :].bitcast(I32))
 
         def v_words(a, jt):
-            return v[a, jt // 4][:, P * (jt % 4) : P * (jt % 4 + 1)].bitcast(FP8X4)
-
-        def gather_scales():
-            gather(v_sc, tab_sc[:], idx, U8, 0, S)
-            for a in range(1, PASSES):
-                w0 = (a - 1) * S // 4
-                nc.scalar.dma_start(
-                    v_sc_moved[0:SHIFT_ROWS, w0 : w0 + S // 4],
-                    v_sc[4 * a : 4 * a + SHIFT_ROWS, :].bitcast(I32),
-                )
+            return v[a][:, P * jt : P * (jt + 1)].bitcast(FP8X4)
 
         def v_scale(a, jt):
             if a == 0:
@@ -125,13 +112,16 @@ def tile_list_pairs_tradable_edge_kernel(
             return v_sc_moved[:].bitcast(U8)[:, c0 : c0 + P]
 
         b_ps = [bank(jt, [P, H], "b%d" % jt) for jt in range(8)]
-        sig_lo = big.tile([P, 4, H], F32, name="sig_lo", offset=35 * KB, align_bytes=64)
-        sig = [sig_lo[:, n, :] for n in range(4)]
-        sig_hi = big.tile([P, 4, H], F32, name="sig_hi", offset=14 * KB, align_bytes=64)
-        sig.extend(sig_hi[:, n, :] for n in range(4))
+        sig = [kept([P, H], F32, "sig%d" % jt) for jt in range(EARLY)]
+        sig.extend(
+            shared.tile([P, H], F32, name="sig%d" % jt, offset=(4 + 2 * (jt - EARLY)) * KB, align_bytes=64) for jt in range(EARLY, 8)
+        )
 
         def permuted(ps):
             return ps[:].rearrange("p (q u e) -> p u q e", u=2, e=2)
+
+        def in_runs(t):
+            return t[:].rearrange("p (u q e) -> p u q e", u=2, e=2)
 
         def b_pass(a, jts):
             for jt in jts:
@@ -147,93 +137,92 @@ def tile_list_pairs_tradable_edge_kernel(
 
         def sigmoid(jts):
             for jt in jts:
-                nc.scalar.activation(sig[jt][:].rearrange("p (u q e) -> p u q e", u=2, e=2), permuted(b_ps[jt]), ACT.Sigmoid)
+                nc.scalar.activation(in_runs(sig[jt]), permuted(b_ps[jt]), ACT.Sigmoid)
 
-        w1_grp = [keep.tile([P, H, 4], BF16, name="w1_grp%d" % a, align_bytes=64) for a in range(PASSES)]
-        w1_q = [big.tile([P, H], U32, name="w1_q0", offset=33 * KB, align_bytes=64)]
-        w1_q.extend(keep.tile([P, H], U32, name="w1_q%d" % a, align_bytes=64) for a in range(1, PASSES))
-        w1_sc = keep.tile([P, PASSES, H], U8, name="w1_sc", align_bytes=64)
+        w1_grp = [kept([P, H, 4], BF16, "w1_grp%d" % a) for a in range(PASSES)]
+        w1_sc = kept([P, PASSES, H], U8, "w1_sc")
 
-        def interleave(a, c0, c1, copy):
+        def round_by_copy(a, c0, c1, copy):
             copy(
                 w1_grp[a][:, c0:c1, :].rearrange("p (c m) i -> p c i m", m=4),
                 w1_raw[a][:, :, c0:c1].rearrange("p i (c m) -> p c i m", m=4),
             )
 
-        def quantize_w1(a):
-            nc.vector.quantize_mx(w1_q[a][:].bitcast(FP8X4), w1_sc[:, a, :], w1_grp[a][:].rearrange("p c i -> p (c i)"))
+        w1_q = {}
 
-        a_ps = [bank(jt, [P, H], "a%d" % jt) for jt in range(8)]
+        def quantize_w1(a, dst):
+            w1_q[a] = dst
+            nc.vector.quantize_mx(dst[:].bitcast(FP8X4), w1_sc[:, a, :], w1_grp[a][:].rearrange("p c i -> p (c i)"))
 
-        def a_pass(a, jts):
-            for jt in jts:
-                nc.tensor.matmul_mx(
-                    a_ps[jt][:],
-                    lhsT=v_words(a, jt),
-                    lhsT_scale=v_scale(a, jt),
-                    rhs=w1_q[a][:].bitcast(FP8X4),
-                    rhs_scale=w1_sc[:, a, :],
-                    start=(a == 0),
-                    stop=(a == PASSES - 1),
-                )
+        a_ps = {}
+
+        def a_pass(a, jt):
+            if a == 0:
+                a_ps[jt] = bank(jt, [P, H], "a%d" % jt)
+            nc.tensor.matmul_mx(
+                a_ps[jt][:],
+                lhsT=v_words(a, jt),
+                lhsT_scale=v_scale(a, jt),
+                rhs=w1_q[a][:].bitcast(FP8X4),
+                rhs_scale=w1_sc[:, a, :],
+                start=(a == 0),
+                stop=(a == PASSES - 1),
+            )
 
         lo_j, hi_j = range(0, 4), range(4, 8)
-        gather(v2_sc, tab2_sc[:], idx2, U8, 0, S2)
-        gather_scales()
-        tab.append(load_table(tab_words[2], T, "tab_2", 1 * KB))
-        gather_words(0, 0)
-        b_pass(0, lo_j)
-        gather_words(0, 1)
-        b_pass(0, hi_j)
-        w1_raw.append(load_w1(1, 33 * KB))
-        w1_raw.append(load_w1(2, 14 * KB))
-        interleave(0, 0, H, nc.scalar.copy)
-        v2_sc_moved = big.tile([P, S2 // 4], I32, name="v2_sc_moved", offset=80 * KB, align_bytes=64)
-        nc.gpsimd.memset(v2_sc_moved[:], 0)
+        gather(v2_sc, tab2_sc, idx2, U8, 0, S2)
+        gather(v_sc, tab_sc, idx, U8, 0, S)
+        move_plane(1)
+        w1_raw = [load_w1(0, kept([P, 4, H], F32, "w1_raw0"))]
+        move_plane(2)
+        w1_raw.append(load_w1(1, kept([P, 4, H], F32, "w1_raw1")))
         for r in range(4):
-            nc.scalar.dma_start(v2_sc_moved[r:P:32, :], v2_sc[8 * r : P : 32, :].bitcast(I32))
-        gather(v1, tab[1], idx, U32, 0, S)
-        tab2 = load_table(tab2_words[0], T2, "tab2", 56 * KB)
-        cost_col = big.tile([P, S2 // P], F32, name="cost_col", offset=1 * KB)
-        b_pass(1, lo_j)
-        interleave(1, 0, H // 2, nc.scalar.copy)
-        gather_words(2, 0)
-        b_pass(2, lo_j)
-        b_pass(1, hi_j)
-        sigmoid(lo_j)
-        gather_words(2, 1)
+            nc.sync.dma_start(v2_sc_moved[r:P:32, :], v2_sc[8 * r : P : 32, :].bitcast(I32))
+        w1_raw.append(load_w1(2, shared.tile([P, 4, H], F32, name="w1_raw2", offset=4 * KB, align_bytes=64)))
+        tab2 = load_words(tab2_words[0], T2, "tab2")
+        cost_col = keep.tile([P, S2 // P], F32, name="cost_col")
         with nc.allow_non_contiguous_dma(reason="one cost a partition and candidate tile"):
             nc.sync.dma_start(cost_col[:], cost.rearrange("(t p) -> p t", p=P))
-        b_pass(2, hi_j)
-        interleave(1, H // 2, H, nc.vector.tensor_copy)
-        quantize_w1(0)
-        quantize_w1(1)
+
+        for a in range(PASSES):
+            gather(v[a], tab[a], idx, U32, 0, HALF)
+            b_pass(a, lo_j)
+            gather(v[a], tab[a], idx, U32, HALF, HALF)
+            b_pass(a, hi_j)
+        round_by_copy(0, 0, H, nc.scalar.copy)
+        sigmoid(range(EARLY))
+        for a in range(2):
+            if a == 1:
+                round_by_copy(a, 0, H, nc.vector.tensor_copy)
+            quantize_w1(a, kept([P, H], U32, "w1_q%d" % a))
+            for jt in range(EARLY):
+                a_pass(a, jt)
+        round_by_copy(2, 0, H // 2, nc.scalar.copy)
+        round_by_copy(2, H // 2, H, nc.vector.tensor_copy)
+        quantize_w1(2, kept([P, H], U32, "w1_q2"))
+        sigmoid(range(EARLY, 8))
         for jt in lo_j:
-            a_pass(0, [jt])
-            a_pass(1, [jt])
-        interleave(2, 0, H, nc.vector.tensor_copy)
-        quantize_w1(2)
-        a_pass(2, lo_j)
+            a_pass(2, jt)
 
-        h_grp = [big.tile([P, HALF, 4], BF16, name="h_grp%d" % u, offset=(92 + 4 * u) * KB, align_bytes=64) for u in range(2)]
-        h_q = keep.tile([P, S], U32, name="h_q", align_bytes=64)
-        h_sc = keep.tile([P, S], U8, name="h_sc", align_bytes=64)
+        h_grp = [shared.tile([P, HALF, 4], BF16, name="h_grp0", offset=12 * KB, align_bytes=64), kept([P, HALF, 4], BF16, "h_grp1")]
+        h_q = kept([P, S], U32, "h_q")
+        h_sc = kept([P, S], U8, "h_sc")
 
-        def gate(pair):
-            h_t = []
-            for jt in (2 * pair, 2 * pair + 1):
-                t = big.tile([P, H], BF16, name="h_t%d" % jt, offset=(88 + jt) * KB, align_bytes=64)
-                nc.vector.tensor_tensor(
-                    t[:].rearrange("p (u q e) -> p u q e", u=2, e=2),
-                    permuted(a_ps[jt]),
-                    sig[jt][:].rearrange("p (u q e) -> p u q e", u=2, e=2),
-                    ALU.mult,
-                )
-                h_t.append(t)
-            ps = bank(2 * pair, [P, 2, 2, P], "h_ps%d" % pair)
+        h_t = {}
+        h_t_at = {4: 12 * KB, 5: 13 * KB, 6: 16 * KB, 7: 18 * KB}
+
+        def gate(jt):
+            if jt in h_t_at:
+                h_t[jt] = shared.tile([P, H], BF16, name="h_t%d" % jt, offset=h_t_at[jt], align_bytes=64)
+            else:
+                h_t[jt] = kept([P, H], BF16, "h_t%d" % jt)
+            nc.vector.tensor_tensor(in_runs(h_t[jt]), permuted(a_ps[jt]), in_runs(sig[jt]), ALU.mult)
+
+        def turn(pair):
+            ps = bank((6, 7, 4, 6)[pair], [P, 2, 2, P], "h_ps%d" % pair)
             for n in range(2):
                 for u in range(2):
-                    nc.tensor.transpose(ps[:, n, u, :], h_t[n][:].bitcast(F32)[:, P * u : P * (u + 1)], ident[:])
+                    nc.tensor.transpose(ps[:, n, u, :], h_t[2 * pair + n][:].bitcast(F32)[:, P * u : P * (u + 1)], ident[:])
             cols = slice(2 * P * (pair % 2), 2 * P * (pair % 2 + 1))
             nc.scalar.copy(
                 h_grp[pair // 2][:, cols, :].rearrange("p j t -> p (j t)").bitcast(F32).rearrange("p (n j u) -> p n j u", n=2, u=2),
@@ -244,48 +233,58 @@ def tile_list_pairs_tradable_edge_kernel(
             cols = slice(HALF * half, HALF * (half + 1))
             nc.vector.quantize_mx(h_q[:, cols].bitcast(FP8X4), h_sc[:, cols], h_grp[half][:].rearrange("p j t -> p (j t)"))
 
-        def edge(it, half, bk, res):
+        res = [keep.tile([P, S], F32, name="res%d" % it) for it in range(8)]
+
+        def edge(it, half, bk):
             cols = slice(HALF * half, HALF * (half + 1))
             z = bank(bk, [P, HALF], "z%d_%d" % (it, half))
             nc.tensor.matmul_mx(
                 z[:],
-                lhsT=cand[it // 4][:, P * (it % 4) : P * (it % 4 + 1)].bitcast(FP8X4),
+                lhsT=cand[:, P * it : P * (it + 1)].bitcast(FP8X4),
                 lhsT_scale=v2_sc_moved[:].bitcast(U8)[:, P * it : P * (it + 1)],
                 rhs=h_q[:, cols].bitcast(FP8X4),
                 rhs_scale=h_sc[:, cols],
                 start=True,
                 stop=True,
             )
-            if (it, half) == (0, 0):
-                mag = big.tile([P, HALF], F32, name="mag_first", offset=100 * KB, align_bytes=64)
+            if half == 0 and it < 2:
+                mag = shared.tile([P, HALF], F32, name="mag_first%d" % it, offset=(16 + 2 * it) * KB, align_bytes=64)
             else:
                 mag = work.tile([P, HALF], F32, tag="mag", name="mag%d_%d" % (it, half))
             nc.scalar.activation(mag[:], z[:], ACT.Abs)
-            nc.vector.tensor_scalar(res, mag[:], cost_col[:, it : it + 1], 0.0, ALU.subtract, ALU.max)
+            nc.vector.tensor_scalar(res[it][:, cols], mag[:], cost_col[:, it : it + 1], 0.0, ALU.subtract, ALU.max)
 
-        res = [keep.tile([P, S], F32, name="res%d" % it) for it in range(8)]
-
-        def edge_half(it, half, bk):
-            cols = slice(HALF * half, HALF * (half + 1))
-            edge(it, half, bk, res[it][:, cols])
+        def store(it, cols):
             nc.sync.dma_start(out[P * it : P * (it + 1), cols], res[it][:, cols])
 
-        gate(0)
-        gate(1)
-        sigmoid(hi_j)
-        nc.vector.tensor_copy(cand[0][:], tab2.bitcast(U32).indirect(idx2[:, 0:32]))
-        quantize_h(0)
+        def edge_and_store(it, half, bk):
+            edge(it, half, bk)
+            store(it, slice(HALF * half, HALF * (half + 1)))
+
+        for pair in range(2):
+            gate(2 * pair)
+            gate(2 * pair + 1)
+            turn(pair)
         for jt in hi_j:
-            for a in range(PASSES):
-                a_pass(a, [jt])
-        edge_half(0, 0, 3)
-        nc.vector.tensor_copy(cand[1][:], tab2.bitcast(U32).indirect(idx2[:, 32:64]))
-        for it in range(1, 4):
-            edge_half(it, 0, (3, 1, 0, 2)[it])
-        gate(2)
-        gate(3)
+            for a in range(2 if jt < EARLY else 0, PASSES):
+                a_pass(a, jt)
+        gather(cand, tab2, idx2, U32, 0, HALF)
+        quantize_h(0)
+        gate(4)
+        gate(5)
+        edge_and_store(0, 0, 0)
+        gate(6)
+        edge_and_store(1, 0, 1)
+        gate(7)
+        edge_and_store(2, 0, 2)
+        turn(2)
+        gather(cand, tab2, idx2, U32, HALF, HALF // 2)
+        edge_and_store(3, 0, 3)
+        turn(3)
         quantize_h(1)
-        for it in range(4, 8):
-            edge_half(it, 0, (3, 1, 0, 2)[it - 4])
-        for it in range(8):
-            edge_half(it, 1, (5, 7, 4, 6, 3, 1, 0, 2)[it])
+        edge_and_store(4, 0, 5)
+        edge_and_store(5, 0, 7)
+        gather(cand, tab2, idx2, U32, 3 * HALF // 2, HALF // 2)
+        rest = [(it, 1) for it in range(6)] + [(it, half) for it in (6, 7) for half in range(2)]
+        for n, (it, half) in enumerate(rest):
+            edge_and_store(it, half, (0, 1, 2, 3, 4, 6, 5, 7)[n % 8])

@@ -20,7 +20,8 @@ ALU = mybir.AluOpType
 P = 128
 PASSES = K // 512
 HALF = 512
-EARLY = 4
+EARLY = 5
+SCALAR_COLS = (320, 0, 192)
 KB = 1024
 
 
@@ -49,13 +50,13 @@ def tile_list_pairs_tradable_edge_kernel(
         v_sc_moved = kept([P, (PASSES - 1) * S // 4], I32, "v_sc_moved")
         v2_sc_moved = kept([P, S2 // 4], I32, "v2_sc_moved")
         ident = kept([P, P], F32, "ident")
-        nc.vector.memset(tab2_sc[:, 0 : T2 // 8], 0)
-        nc.gpsimd.memset(tab2_sc[:, T2 // 8 : T2 // 4], 0)
+        nc.vector.memset(tab2_sc[:], 0)
         nc.vector.memset(tab_sc[:], 0)
         nc.vector.memset(w4_sc[:], 0)
         nc.vector.memset(v_sc_moved[:], 0)
-        nc.gpsimd.memset(v2_sc_moved[:], 0)
-        make_identity(nc, ident[:])
+        nc.vector.memset(v2_sc_moved[:], 0)
+        nc.vector.memset(ident[:], 0.0)
+        make_identity(nc, ident[:], nomemset=True)
 
         def load_words(src, width, name):
             t = kept([P, width], I32, name)
@@ -68,9 +69,9 @@ def tile_list_pairs_tradable_edge_kernel(
 
         tab_0 = kept([P, T], I32, "tab_0")
         tab_0_src = tab_words[0].rearrange("p t i -> p (t i)").bitcast(I32)
+        nc.sync.dma_start(tab_0[:, 0 : 3 * T // 8], tab_0_src[:, 0 : 3 * T // 8])
         nc.sync.dma_start(idx2[:], offs2)
         nc.sync.dma_start(idx[:], offs)
-        nc.sync.dma_start(tab_0[:, 0 : 3 * T // 8], tab_0_src[:, 0 : 3 * T // 8])
         nc.sync.dma_start(tab2_sc[0:P:8, :], tab2_scales[0].bitcast(I32))
         nc.sync.dma_start(tab_0[:, 3 * T // 8 : T], tab_0_src[:, 3 * T // 8 : T])
         for r in range(4):
@@ -92,7 +93,7 @@ def tile_list_pairs_tradable_edge_kernel(
         v_sc = kept([P, S], U8, "v_sc")
         v2_sc = kept([P, S2], U8, "v2_sc")
         v = [shared.tile([P, S], U32, name="v0", offset=0, align_bytes=64), kept([P, S], U32, "v1"), kept([P, S], U32, "v2")]
-        cand = kept([P, S2], U32, "cand")
+        cand = {}
 
         def gather(dst, window, lst, dt, lo, n):
             nc.vector.tensor_copy(dst[:, lo : lo + n], window[:].bitcast(dt).indirect(lst[:, lo // 16 : (lo + n) // 16]))
@@ -101,6 +102,11 @@ def tile_list_pairs_tradable_edge_kernel(
             w0 = (a - 1) * S // 4
             for r in range(4):
                 nc.sync.dma_start(v_sc_moved[r:P:32, w0 : w0 + S // 4], v_sc[8 * r + 3 + a : P : 32, :].bitcast(I32))
+
+        def gather_cand(first, count, t):
+            nc.vector.tensor_copy(t[:], tab2[:].bitcast(U32).indirect(idx2[:, 8 * first : 8 * (first + count)]))
+            for n in range(count):
+                cand[first + n] = t[:, P * n : P * (n + 1)]
 
         def v_words(a, jt):
             return v[a][:, P * jt : P * (jt + 1)].bitcast(FP8X4)
@@ -176,10 +182,10 @@ def tile_list_pairs_tradable_edge_kernel(
         w1_raw = [load_w1(0, kept([P, 4, H], F32, "w1_raw0"))]
         move_plane(2)
         w1_raw.append(load_w1(1, kept([P, 4, H], F32, "w1_raw1")))
-        for r in range(4):
-            nc.sync.dma_start(v2_sc_moved[r:P:32, :], v2_sc[8 * r : P : 32, :].bitcast(I32))
         w1_raw.append(load_w1(2, shared.tile([P, 4, H], F32, name="w1_raw2", offset=4 * KB, align_bytes=64)))
         tab2 = load_words(tab2_words[0], T2, "tab2")
+        for r in range(4):
+            nc.sync.dma_start(v2_sc_moved[r:P:32, :], v2_sc[8 * r : P : 32, :].bitcast(I32))
         cost_col = keep.tile([P, S2 // P], F32, name="cost_col")
         with nc.allow_non_contiguous_dma(reason="one cost a partition and candidate tile"):
             nc.sync.dma_start(cost_col[:], cost.rearrange("(t p) -> p t", p=P))
@@ -189,22 +195,21 @@ def tile_list_pairs_tradable_edge_kernel(
             b_pass(a, lo_j)
             gather(v[a], tab[a], idx, U32, HALF, HALF)
             b_pass(a, hi_j)
-        round_by_copy(0, 0, H, nc.scalar.copy)
+        round_by_copy(0, 0, SCALAR_COLS[0], nc.scalar.copy)
         sigmoid(range(EARLY))
         for a in range(2):
-            if a == 1:
-                round_by_copy(a, 0, H, nc.vector.tensor_copy)
+            round_by_copy(a, SCALAR_COLS[a], H, nc.vector.tensor_copy)
             quantize_w1(a, kept([P, H], U32, "w1_q%d" % a))
             for jt in range(EARLY):
                 a_pass(a, jt)
-        round_by_copy(2, 0, H // 2, nc.scalar.copy)
-        round_by_copy(2, H // 2, H, nc.vector.tensor_copy)
+        round_by_copy(2, 0, SCALAR_COLS[2], nc.scalar.copy)
+        round_by_copy(2, SCALAR_COLS[2], H, nc.vector.tensor_copy)
         quantize_w1(2, kept([P, H], U32, "w1_q2"))
         sigmoid(range(EARLY, 8))
         for jt in lo_j:
             a_pass(2, jt)
 
-        h_grp = [shared.tile([P, HALF, 4], BF16, name="h_grp0", offset=12 * KB, align_bytes=64), kept([P, HALF, 4], BF16, "h_grp1")]
+        h_grp = [shared.tile([P, HALF, 4], BF16, name="h_grp0", offset=12 * KB, align_bytes=64), shared.tile([P, HALF, 4], BF16, name="h_grp1", offset=30 * KB, align_bytes=64)]
         h_q = kept([P, S], U32, "h_q")
         h_sc = kept([P, S], U8, "h_sc")
 
@@ -218,14 +223,14 @@ def tile_list_pairs_tradable_edge_kernel(
                 h_t[jt] = kept([P, H], BF16, "h_t%d" % jt)
             nc.vector.tensor_tensor(in_runs(h_t[jt]), permuted(a_ps[jt]), in_runs(sig[jt]), ALU.mult)
 
-        def turn(pair):
-            ps = bank((6, 7, 4, 6)[pair], [P, 2, 2, P], "h_ps%d" % pair)
-            for n in range(2):
+        def turn(first, count, bk):
+            ps = bank(bk, [P, count, 2, P], "h_ps%d" % first)
+            for n in range(count):
                 for u in range(2):
-                    nc.tensor.transpose(ps[:, n, u, :], h_t[2 * pair + n][:].bitcast(F32)[:, P * u : P * (u + 1)], ident[:])
-            cols = slice(2 * P * (pair % 2), 2 * P * (pair % 2 + 1))
+                    nc.tensor.transpose(ps[:, n, u, :], h_t[first + n][:].bitcast(F32)[:, P * u : P * (u + 1)], ident[:])
+            cols = slice(P * (first % 4), P * (first % 4 + count))
             nc.scalar.copy(
-                h_grp[pair // 2][:, cols, :].rearrange("p j t -> p (j t)").bitcast(F32).rearrange("p (n j u) -> p n j u", n=2, u=2),
+                h_grp[first // 4][:, cols, :].rearrange("p j t -> p (j t)").bitcast(F32).rearrange("p (n j u) -> p n j u", n=count, u=2),
                 ps[:].rearrange("p n u j -> p n j u"),
             )
 
@@ -240,15 +245,15 @@ def tile_list_pairs_tradable_edge_kernel(
             z = bank(bk, [P, HALF], "z%d_%d" % (it, half))
             nc.tensor.matmul_mx(
                 z[:],
-                lhsT=cand[:, P * it : P * (it + 1)].bitcast(FP8X4),
+                lhsT=cand[it].bitcast(FP8X4),
                 lhsT_scale=v2_sc_moved[:].bitcast(U8)[:, P * it : P * (it + 1)],
                 rhs=h_q[:, cols].bitcast(FP8X4),
                 rhs_scale=h_sc[:, cols],
                 start=True,
                 stop=True,
             )
-            if half == 0 and it < 2:
-                mag = shared.tile([P, HALF], F32, name="mag_first%d" % it, offset=(16 + 2 * it) * KB, align_bytes=64)
+            if half == 0 and it < 3:
+                mag = shared.tile([P, HALF], F32, name="mag_first%d" % it, offset=(16, 18, 28)[it] * KB, align_bytes=64)
             else:
                 mag = work.tile([P, HALF], F32, tag="mag", name="mag%d_%d" % (it, half))
             nc.scalar.activation(mag[:], z[:], ACT.Abs)
@@ -261,30 +266,36 @@ def tile_list_pairs_tradable_edge_kernel(
             edge(it, half, bk)
             store(it, slice(HALF * half, HALF * (half + 1)))
 
-        for pair in range(2):
-            gate(2 * pair)
-            gate(2 * pair + 1)
-            turn(pair)
-        for jt in hi_j:
+        gate(0)
+        gate(1)
+        turn(0, 2, 0)
+        gate(2)
+        turn(2, 1, 6)
+        gate(3)
+        turn(3, 1, 7)
+        for jt in range(4, 7):
             for a in range(2 if jt < EARLY else 0, PASSES):
                 a_pass(a, jt)
-        gather(cand, tab2, idx2, U32, 0, HALF)
+        gather_cand(0, 4, kept([P, HALF], U32, "cand0"))
         quantize_h(0)
         gate(4)
         gate(5)
-        edge_and_store(0, 0, 0)
+        edge_and_store(0, 0, 7)
+        for a in range(PASSES):
+            a_pass(a, 7)
         gate(6)
         edge_and_store(1, 0, 1)
+        turn(4, 2, 1)
         gate(7)
         edge_and_store(2, 0, 2)
-        turn(2)
-        gather(cand, tab2, idx2, U32, HALF, HALF // 2)
+        turn(6, 1, 6)
+        gather_cand(4, 2, shared.tile([P, 2 * P], U32, name="cand4", offset=28 * KB, align_bytes=64))
         edge_and_store(3, 0, 3)
-        turn(3)
+        turn(7, 1, 5)
         quantize_h(1)
-        edge_and_store(4, 0, 5)
-        edge_and_store(5, 0, 7)
-        gather(cand, tab2, idx2, U32, 3 * HALF // 2, HALF // 2)
+        edge_and_store(4, 0, 0)
+        edge_and_store(5, 0, 4)
+        gather_cand(6, 2, shared.tile([P, 2 * P], U32, name="cand6", offset=30 * KB, align_bytes=64))
         rest = [(it, 1) for it in range(6)] + [(it, half) for it in (6, 7) for half in range(2)]
         for n, (it, half) in enumerate(rest):
-            edge_and_store(it, half, (0, 1, 2, 3, 4, 6, 5, 7)[n % 8])
+            edge_and_store(it, half, (2, 3, 7, 1, 6, 5, 0, 4)[n % 8])

@@ -20,8 +20,8 @@ ALU = mybir.AluOpType
 P = 128
 PASSES = K // 512
 HALF = 512
-EARLY = 5
-SCALAR_COLS = (320, 0, 192)
+EARLY = 4
+SCALAR_COLS = (320, 0, 112)
 KB = 1024
 
 
@@ -69,11 +69,11 @@ def tile_list_pairs_tradable_edge_kernel(
 
         tab_0 = kept([P, T], I32, "tab_0")
         tab_0_src = tab_words[0].rearrange("p t i -> p (t i)").bitcast(I32)
-        nc.sync.dma_start(tab_0[:, 0 : 3 * T // 8], tab_0_src[:, 0 : 3 * T // 8])
+        nc.sync.dma_start(tab_0[:, 0 : T // 4], tab_0_src[:, 0 : T // 4])
         nc.sync.dma_start(idx2[:], offs2)
         nc.sync.dma_start(idx[:], offs)
         nc.sync.dma_start(tab2_sc[0:P:8, :], tab2_scales[0].bitcast(I32))
-        nc.sync.dma_start(tab_0[:, 3 * T // 8 : T], tab_0_src[:, 3 * T // 8 : T])
+        nc.sync.dma_start(tab_0[:, T // 4 : T], tab_0_src[:, T // 4 : T])
         for r in range(4):
             nc.sync.dma_start(tab_sc[r:P:32, :], tab_scales[0, r:16:4, :].bitcast(I32))
         for a in range(1, PASSES):
@@ -82,12 +82,12 @@ def tile_list_pairs_tradable_edge_kernel(
         warm = keep.tile([P, 1], F32, name="warm")
         nc.scalar.activation(warm[:], ident[:, 0:1], ACT.Sigmoid)
         w4 = kept([P, PASSES, H // 2], I32, "w4")
-        nc.sync.dma_start(w4[:], w4_words.bitcast(I32).rearrange("a p c -> p a c"))
         for r in range(4):
             nc.sync.dma_start(
                 w4_sc[r:P:32, :].rearrange("p (a c) -> p a c", a=PASSES),
                 w4_scales[:, r:16:4, :].bitcast(I32).rearrange("a q c -> q a c"),
             )
+        nc.sync.dma_start(w4[:], w4_words.bitcast(I32).rearrange("a p c -> p a c"))
         tab.append(load_words(tab_words[2], T, "tab_2"))
 
         v_sc = kept([P, S], U8, "v_sc")
@@ -156,23 +156,23 @@ def tile_list_pairs_tradable_edge_kernel(
 
         w1_q = {}
 
-        def quantize_w1(a, dst):
+        def quantize_w1(a, dst, cols=slice(0, H)):
             w1_q[a] = dst
-            nc.vector.quantize_mx(dst[:].bitcast(FP8X4), w1_sc[:, a, :], w1_grp[a][:].rearrange("p c i -> p (c i)"))
+            nc.vector.quantize_mx(dst[:, cols].bitcast(FP8X4), w1_sc[:, a, cols], w1_grp[a][:, cols, :].rearrange("p c i -> p (c i)"))
 
         a_ps = {}
 
-        def a_pass(a, jt):
+        def a_pass(a, jt, cols=slice(0, H)):
             if a == 0:
                 a_ps[jt] = bank(jt, [P, H], "a%d" % jt)
             nc.tensor.matmul_mx(
-                a_ps[jt][:],
+                a_ps[jt][:, cols],
                 lhsT=v_words(a, jt),
                 lhsT_scale=v_scale(a, jt),
-                rhs=w1_q[a][:].bitcast(FP8X4),
-                rhs_scale=w1_sc[:, a, :],
+                rhs=w1_q[a][:, cols].bitcast(FP8X4),
+                rhs_scale=w1_sc[:, a, cols],
                 start=(a == 0),
-                stop=(a == PASSES - 1),
+                stop=(a == PASSES - 1 and cols.stop == H),
             )
 
         lo_j, hi_j = range(0, 4), range(4, 8)
@@ -202,19 +202,24 @@ def tile_list_pairs_tradable_edge_kernel(
             quantize_w1(a, kept([P, H], U32, "w1_q%d" % a))
             for jt in range(EARLY):
                 a_pass(a, jt)
-        round_by_copy(2, 0, SCALAR_COLS[2], nc.scalar.copy)
-        round_by_copy(2, SCALAR_COLS[2], H, nc.vector.tensor_copy)
-        quantize_w1(2, kept([P, H], U32, "w1_q2"))
+        halves = (slice(0, H // 2), slice(H // 2, H))
+        for cols in halves:
+            round_by_copy(2, cols.start, cols.start + SCALAR_COLS[2], nc.scalar.copy)
+            round_by_copy(2, cols.start + SCALAR_COLS[2], cols.stop, nc.vector.tensor_copy)
+        w1_q2 = kept([P, H], U32, "w1_q2")
+        for cols in halves:
+            quantize_w1(2, w1_q2, cols)
         sigmoid(range(EARLY, 8))
         for jt in lo_j:
-            a_pass(2, jt)
+            for cols in halves:
+                a_pass(2, jt, cols)
 
         h_grp = [shared.tile([P, HALF, 4], BF16, name="h_grp0", offset=12 * KB, align_bytes=64), shared.tile([P, HALF, 4], BF16, name="h_grp1", offset=30 * KB, align_bytes=64)]
         h_q = kept([P, S], U32, "h_q")
         h_sc = kept([P, S], U8, "h_sc")
 
         h_t = {}
-        h_t_at = {4: 12 * KB, 5: 13 * KB, 6: 16 * KB, 7: 18 * KB}
+        h_t_at = {5: 13 * KB, 6: 16 * KB, 7: 18 * KB}
 
         def gate(jt):
             if jt in h_t_at:
@@ -270,16 +275,17 @@ def tile_list_pairs_tradable_edge_kernel(
         gate(1)
         turn(0, 2, 0)
         gate(2)
-        turn(2, 1, 6)
+        turn(2, 1, 5)
         gate(3)
-        turn(3, 1, 7)
+        turn(3, 1, 6)
         for jt in range(4, 7):
-            for a in range(2 if jt < EARLY else 0, PASSES):
+            for a in range(PASSES):
                 a_pass(a, jt)
         gather_cand(0, 4, kept([P, HALF], U32, "cand0"))
         quantize_h(0)
         gate(4)
         gate(5)
+        gather_cand(4, 2, shared.tile([P, 2 * P], U32, name="cand4", offset=14 * KB, align_bytes=64))
         edge_and_store(0, 0, 7)
         for a in range(PASSES):
             a_pass(a, 7)
@@ -287,15 +293,13 @@ def tile_list_pairs_tradable_edge_kernel(
         edge_and_store(1, 0, 1)
         turn(4, 2, 1)
         gate(7)
-        edge_and_store(2, 0, 2)
         turn(6, 1, 6)
-        gather_cand(4, 2, shared.tile([P, 2 * P], U32, name="cand4", offset=28 * KB, align_bytes=64))
+        edge_and_store(2, 0, 2)
+        gather_cand(6, 2, shared.tile([P, 2 * P], U32, name="cand6", offset=28 * KB, align_bytes=64))
         edge_and_store(3, 0, 3)
         turn(7, 1, 5)
         quantize_h(1)
-        edge_and_store(4, 0, 0)
-        edge_and_store(5, 0, 4)
-        gather_cand(6, 2, shared.tile([P, 2 * P], U32, name="cand6", offset=30 * KB, align_bytes=64))
-        rest = [(it, 1) for it in range(6)] + [(it, half) for it in (6, 7) for half in range(2)]
-        for n, (it, half) in enumerate(rest):
-            edge_and_store(it, half, (2, 3, 7, 1, 6, 5, 0, 4)[n % 8])
+        for it in range(4, 8):
+            edge_and_store(it, 0, (0, 4, 2, 3)[it - 4])
+        for it in range(8):
+            edge_and_store(it, 1, (7, 1, 6, 5, 0, 4, 2, 3)[it])

@@ -215,7 +215,7 @@ def tile_list_pairs_tradable_edge_kernel(
                 a_pass(2, jt, cols)
 
         h_grp = [shared.tile([P, HALF, 4], BF16, name="h_grp0", offset=12 * KB, align_bytes=64), shared.tile([P, HALF, 4], BF16, name="h_grp1", offset=30 * KB, align_bytes=64)]
-        h_q = kept([P, S], U32, "h_q")
+        h_q = [kept([P, HALF], U32, "h_q0"), shared.tile([P, HALF], U32, name="h_q1", offset=34 * KB, align_bytes=64)]
         h_sc = kept([P, S], U8, "h_sc")
 
         h_t = {}
@@ -241,9 +241,11 @@ def tile_list_pairs_tradable_edge_kernel(
 
         def quantize_h(half):
             cols = slice(HALF * half, HALF * (half + 1))
-            nc.vector.quantize_mx(h_q[:, cols].bitcast(FP8X4), h_sc[:, cols], h_grp[half][:].rearrange("p j t -> p (j t)"))
+            nc.vector.quantize_mx(h_q[half][:].bitcast(FP8X4), h_sc[:, cols], h_grp[half][:].rearrange("p j t -> p (j t)"))
 
         res = [keep.tile([P, S], F32, name="res%d" % it) for it in range(8)]
+
+        mag_at = {0: 16 * KB, 1: 18 * KB, 3: 28 * KB, 4: 34 * KB}
 
         def edge(it, half, bk):
             cols = slice(HALF * half, HALF * (half + 1))
@@ -252,13 +254,13 @@ def tile_list_pairs_tradable_edge_kernel(
                 z[:],
                 lhsT=cand[it].bitcast(FP8X4),
                 lhsT_scale=v2_sc_moved[:].bitcast(U8)[:, P * it : P * (it + 1)],
-                rhs=h_q[:, cols].bitcast(FP8X4),
+                rhs=h_q[half][:].bitcast(FP8X4),
                 rhs_scale=h_sc[:, cols],
                 start=True,
                 stop=True,
             )
-            if half == 0 and it < 3:
-                mag = shared.tile([P, HALF], F32, name="mag_first%d" % it, offset=(16, 18, 28)[it] * KB, align_bytes=64)
+            if half == 0 and it in mag_at:
+                mag = shared.tile([P, HALF], F32, name="mag_first%d" % it, offset=mag_at[it], align_bytes=64)
             else:
                 mag = work.tile([P, HALF], F32, tag="mag", name="mag%d_%d" % (it, half))
             nc.scalar.activation(mag[:], z[:], ACT.Abs)
@@ -295,11 +297,12 @@ def tile_list_pairs_tradable_edge_kernel(
         gate(7)
         turn(6, 1, 6)
         edge_and_store(2, 0, 2)
-        gather_cand(6, 2, shared.tile([P, 2 * P], U32, name="cand6", offset=28 * KB, align_bytes=64))
         edge_and_store(3, 0, 3)
+        gather_cand(6, 2, shared.tile([P, 2 * P], U32, name="cand6", offset=28 * KB, align_bytes=64))
+        edge_and_store(4, 0, 0)
         turn(7, 1, 5)
         quantize_h(1)
-        for it in range(4, 8):
-            edge_and_store(it, 0, (0, 4, 2, 3)[it - 4])
+        for it in range(5, 8):
+            edge_and_store(it, 0, (4, 2, 3)[it - 5])
         for it in range(8):
             edge_and_store(it, 1, (7, 1, 6, 5, 0, 4, 2, 3)[it])

@@ -197,12 +197,18 @@ def tile_list_pairs_tradable_edge_kernel(
             b_pass(a, hi_j)
         round_by_copy(0, 0, SCALAR_COLS[0], nc.scalar.copy)
         sigmoid(range(EARLY))
-        for a in range(2):
-            round_by_copy(a, SCALAR_COLS[a], H, nc.vector.tensor_copy)
-            quantize_w1(a, kept([P, H], U32, "w1_q%d" % a))
-            for jt in range(EARLY):
-                a_pass(a, jt)
         halves = (slice(0, H // 2), slice(H // 2, H))
+        round_by_copy(0, SCALAR_COLS[0], H, nc.vector.tensor_copy)
+        quantize_w1(0, kept([P, H], U32, "w1_q0"))
+        for jt in range(EARLY):
+            a_pass(0, jt)
+        for cols in halves:
+            round_by_copy(1, cols.start, cols.stop, nc.vector.tensor_copy)
+        w1_q1 = kept([P, H], U32, "w1_q1")
+        for cols in halves:
+            quantize_w1(1, w1_q1, cols)
+        for jt in range(EARLY):
+            a_pass(1, jt)
         for cols in halves:
             round_by_copy(2, cols.start, cols.start + SCALAR_COLS[2], nc.scalar.copy)
             round_by_copy(2, cols.start + SCALAR_COLS[2], cols.stop, nc.vector.tensor_copy)
@@ -219,7 +225,7 @@ def tile_list_pairs_tradable_edge_kernel(
         h_sc = kept([P, S], U8, "h_sc")
 
         h_t = {}
-        h_t_at = {5: 13 * KB, 6: 16 * KB, 7: 18 * KB}
+        h_t_at = {6: 13 * KB, 7: 18 * KB}
 
         def gate(jt):
             if jt in h_t_at:
@@ -227,6 +233,12 @@ def tile_list_pairs_tradable_edge_kernel(
             else:
                 h_t[jt] = kept([P, H], BF16, "h_t%d" % jt)
             nc.vector.tensor_tensor(in_runs(h_t[jt]), permuted(a_ps[jt]), in_runs(sig[jt]), ALU.mult)
+
+        def gate_on_gpsimd(jt):
+            a_sb = kept([P, H], F32, "a_sb%d" % jt)
+            h_t[jt] = kept([P, H], BF16, "h_t%d" % jt)
+            nc.scalar.copy(in_runs(a_sb), permuted(a_ps[jt]))
+            nc.gpsimd.tensor_tensor(h_t[jt][:], a_sb[:], sig[jt][:], ALU.mult)
 
         def turn(first, count, bk):
             ps = bank(bk, [P, count, 2, P], "h_ps%d" % first)
@@ -245,9 +257,9 @@ def tile_list_pairs_tradable_edge_kernel(
 
         res = [keep.tile([P, S], F32, name="res%d" % it) for it in range(8)]
 
-        mag_at = {0: 16 * KB, 1: 18 * KB, 3: 28 * KB, 4: 34 * KB}
+        mag_at = {1: 18 * KB, 3: 28 * KB, 4: 34 * KB}
 
-        def edge(it, half, bk):
+        def edge_and_store(it, half, bk, pieces=1):
             cols = slice(HALF * half, HALF * (half + 1))
             z = bank(bk, [P, HALF], "z%d_%d" % (it, half))
             nc.tensor.matmul_mx(
@@ -263,15 +275,15 @@ def tile_list_pairs_tradable_edge_kernel(
                 mag = shared.tile([P, HALF], F32, name="mag_first%d" % it, offset=mag_at[it], align_bytes=64)
             else:
                 mag = work.tile([P, HALF], F32, tag="mag", name="mag%d_%d" % (it, half))
-            nc.scalar.activation(mag[:], z[:], ACT.Abs)
-            nc.vector.tensor_scalar(res[it][:, cols], mag[:], cost_col[:, it : it + 1], 0.0, ALU.subtract, ALU.max)
+            width = HALF // pieces
+            for c0 in range(0, HALF, width):
+                part = slice(cols.start + c0, cols.start + c0 + width)
+                nc.scalar.activation(mag[:, c0 : c0 + width], z[:, c0 : c0 + width], ACT.Abs)
+                nc.vector.tensor_scalar(res[it][:, part], mag[:, c0 : c0 + width], cost_col[:, it : it + 1], 0.0, ALU.subtract, ALU.max)
+                store(it, part)
 
         def store(it, cols):
             nc.sync.dma_start(out[P * it : P * (it + 1), cols], res[it][:, cols])
-
-        def edge_and_store(it, half, bk):
-            edge(it, half, bk)
-            store(it, slice(HALF * half, HALF * (half + 1)))
 
         gate(0)
         gate(1)
@@ -283,26 +295,27 @@ def tile_list_pairs_tradable_edge_kernel(
         for jt in range(4, 7):
             for a in range(PASSES):
                 a_pass(a, jt)
-        gather_cand(0, 4, kept([P, HALF], U32, "cand0"))
+        gather_cand(0, 2, kept([P, 2 * P], U32, "cand0"))
         quantize_h(0)
         gate(4)
-        gate(5)
+        gather_cand(2, 2, shared.tile([P, 2 * P], U32, name="cand2", offset=12 * KB, align_bytes=64))
+        gate_on_gpsimd(5)
         gather_cand(4, 2, shared.tile([P, 2 * P], U32, name="cand4", offset=14 * KB, align_bytes=64))
+        gate(6)
         edge_and_store(0, 0, 7)
         for a in range(PASSES):
             a_pass(a, 7)
-        gate(6)
         edge_and_store(1, 0, 1)
         turn(4, 2, 1)
         gate(7)
-        turn(6, 1, 6)
         edge_and_store(2, 0, 2)
+        turn(6, 1, 2)
         edge_and_store(3, 0, 3)
         gather_cand(6, 2, shared.tile([P, 2 * P], U32, name="cand6", offset=28 * KB, align_bytes=64))
         edge_and_store(4, 0, 0)
         turn(7, 1, 5)
         quantize_h(1)
         for it in range(5, 8):
-            edge_and_store(it, 0, (4, 2, 3)[it - 5])
+            edge_and_store(it, 0, (4, 6, 3)[it - 5])
         for it in range(8):
-            edge_and_store(it, 1, (7, 1, 6, 5, 0, 4, 2, 3)[it])
+            edge_and_store(it, 1, (7, 1, 2, 5, 0, 4, 6, 3)[it], 2 if it == 7 else 1)

@@ -240,13 +240,13 @@ def tile_list_pairs_tradable_edge_kernel(
             nc.scalar.copy(in_runs(a_sb), permuted(a_ps[jt]))
             nc.gpsimd.tensor_tensor(h_t[jt][:], a_sb[:], sig[jt][:], ALU.mult)
 
-        def turn(first, count, bk):
+        def turn(first, count, bk, copy=nc.scalar.copy):
             ps = bank(bk, [P, count, 2, P], "h_ps%d" % first)
             for n in range(count):
                 for u in range(2):
                     nc.tensor.transpose(ps[:, n, u, :], h_t[first + n][:].bitcast(F32)[:, P * u : P * (u + 1)], ident[:])
             cols = slice(P * (first % 4), P * (first % 4 + count))
-            nc.scalar.copy(
+            copy(
                 h_grp[first // 4][:, cols, :].rearrange("p j t -> p (j t)").bitcast(F32).rearrange("p (n j u) -> p n j u", n=count, u=2),
                 ps[:].rearrange("p n u j -> p n j u"),
             )
@@ -257,7 +257,7 @@ def tile_list_pairs_tradable_edge_kernel(
 
         res = [keep.tile([P, S], F32, name="res%d" % it) for it in range(8)]
 
-        mag_at = {1: 18 * KB, 3: 28 * KB, 4: 34 * KB}
+        mag_at = {1: 18 * KB, 4: 34 * KB}
 
         def edge_and_store(it, half, bk, pieces=1):
             cols = slice(HALF * half, HALF * (half + 1))
@@ -287,20 +287,21 @@ def tile_list_pairs_tradable_edge_kernel(
 
         gate(0)
         gate(1)
+        for a in range(PASSES):
+            a_pass(a, 4)
+        gate_on_gpsimd(4)
         turn(0, 2, 0)
         gate(2)
         turn(2, 1, 5)
         gate(3)
         turn(3, 1, 6)
-        for jt in range(4, 7):
+        for jt in range(5, 7):
             for a in range(PASSES):
                 a_pass(a, jt)
-        gather_cand(0, 2, kept([P, 2 * P], U32, "cand0"))
+        gather_cand(0, 4, kept([P, 4 * P], U32, "cand0"))
         quantize_h(0)
-        gate(4)
-        gather_cand(2, 2, shared.tile([P, 2 * P], U32, name="cand2", offset=12 * KB, align_bytes=64))
         gate_on_gpsimd(5)
-        gather_cand(4, 2, shared.tile([P, 2 * P], U32, name="cand4", offset=14 * KB, align_bytes=64))
+        gather_cand(4, 4, shared.tile([P, 4 * P], U32, name="cand4", offset=14 * KB, align_bytes=64))
         gate(6)
         edge_and_store(0, 0, 7)
         for a in range(PASSES):
@@ -309,11 +310,10 @@ def tile_list_pairs_tradable_edge_kernel(
         turn(4, 2, 1)
         gate(7)
         edge_and_store(2, 0, 2)
-        turn(6, 1, 2)
+        turn(6, 1, 2, nc.vector.tensor_copy)
         edge_and_store(3, 0, 3)
-        gather_cand(6, 2, shared.tile([P, 2 * P], U32, name="cand6", offset=28 * KB, align_bytes=64))
+        turn(7, 1, 5, nc.vector.tensor_copy)
         edge_and_store(4, 0, 0)
-        turn(7, 1, 5)
         quantize_h(1)
         for it in range(5, 8):
             edge_and_store(it, 0, (4, 6, 3)[it - 5])

from contextlib import ExitStack

import concourse.mybir as mybir
from concourse.masks import make_identity

K, T, S, H, T2, S2 = 1536, 2048, 1024, 512, 4096, 1024
FLOPS = 2 * (2 * K * H * S + H * S2 * S)

F32 = mybir.dt.float32
BF16 = mybir.dt.bfloat16
I32 = mybir.dt.int32
U32 = mybir.dt.uint32
U16 = mybir.dt.uint16
U8 = mybir.dt.uint8
FP8X4 = mybir.dt.float8_e4m3fn_x4
FP4X4 = mybir.dt.float4_e2m1fn_x4
ACT = mybir.ActivationFunctionType
ALU = mybir.AluOpType

P = 128
PASSES = K // 512
HALF = 512
EARLY = 4
SCALAR_COLS = (320, 0, 112)
KB = 1024


def tile_list_pairs_tradable_edge_kernel(
    tc, tab_words, tab_scales, offs, tab2_words, tab2_scales, offs2, w1, w4_words, w4_scales, cost, out
):
    nc = tc.nc
    with ExitStack() as ctx:
        keep = ctx.enter_context(tc.tile_pool(name="keep", bufs=1))
        shared = ctx.enter_context(tc.tile_pool(name="shared", bufs=1))
        work = ctx.enter_context(tc.tile_pool(name="work", bufs=8))
        psum = ctx.enter_context(tc.psum_pool(name="psum", bufs=1))

        def bank(n, shape, name):
            return psum.tile(shape, F32, tag="bank%d" % n, name=name)

        def kept(shape, dt, name):
            return keep.tile(shape, dt, name=name, align_bytes=64)

        idx = keep.tile([P, S // 16], U16, name="idx")
        idx2 = keep.tile([P, S2 // 16], U16, name="idx2")

        tab_sc = shared.tile([P, T // 4], I32, name="tab_sc", offset=0, align_bytes=64)
        w4_sc = kept([P, PASSES * H // 4], I32, "w4_sc")
        tab2_sc = kept([P, T2 // 4], I32, "tab2_sc")
        v_sc_moved = kept([P, (PASSES - 1) * S // 4], I32, "v_sc_moved")
        v2_sc_moved = kept([P, S2 // 4], I32, "v2_sc_moved")
        ident = kept([P, P], F32, "ident")
        nc.vector.memset(tab2_sc[:], 0)
        nc.vector.memset(tab_sc[:], 0)
        nc.vector.memset(w4_sc[:], 0)
        nc.vector.memset(v_sc_moved[:], 0)
        nc.vector.memset(v2_sc_moved[:], 0)
        nc.vector.memset(ident[:], 0.0)
        make_identity(nc, ident[:], nomemset=True)

        def load_words(src, width, name):
            t = kept([P, width], I32, name)
            nc.sync.dma_start(t[:], src.rearrange("p t i -> p (t i)").bitcast(I32))
            return t

        def load_w1(a, t):
            nc.sync.dma_start(t[:], w1[512 * a : 512 * (a + 1), :].rearrange("(p i) r -> p i r", i=4))
            return t

        tab_0 = kept([P, T], I32, "tab_0")
        tab_0_src = tab_words[0].rearrange("p t i -> p (t i)").bitcast(I32)
        nc.sync.dma_start(tab_0[:, 0 : T // 4], tab_0_src[:, 0 : T // 4])
        nc.sync.dma_start(idx2[:], offs2)
        nc.sync.dma_start(idx[:], offs)
        nc.sync.dma_start(tab2_sc[0:P:8, :], tab2_scales[0].bitcast(I32))
        nc.sync.dma_start(tab_0[:, T // 4 : T], tab_0_src[:, T // 4 : T])
        for r in range(4):
            nc.sync.dma_start(tab_sc[r:P:32, :], tab_scales[0, r:16:4, :].bitcast(I32))
        for a in range(1, PASSES):
            nc.sync.dma_start(tab_sc[3 + a : P : 8, :], tab_scales[a].bitcast(I32))
        tab = [tab_0, load_words(tab_words[1], T, "tab_1")]
        warm = keep.tile([P, 1], F32, name="warm")
        nc.scalar.activation(warm[:], ident[:, 0:1], ACT.Sigmoid)
        w4 = kept([P, PASSES, H // 2], I32, "w4")
        for r in range(4):
            nc.sync.dma_start(
                w4_sc[r:P:32, :].rearrange("p (a c) -> p a c", a=PASSES),
                w4_scales[:, r:16:4, :].bitcast(I32).rearrange("a q c -> q a c"),
            )
        nc.sync.dma_start(w4[:], w4_words.bitcast(I32).rearrange("a p c -> p a c"))
        tab.append(load_words(tab_words[2], T, "tab_2"))

        v_sc = kept([P, S], U8, "v_sc")
        v2_sc = kept([P, S2], U8, "v2_sc")
        v = [shared.tile([P, S], U32, name="v0", offset=0, align_bytes=64), kept([P, S], U32, "v1"), kept([P, S], U32, "v2")]
        cand = {}

        def gather(dst, window, lst, dt, lo, n):
            nc.vector.tensor_copy(dst[:, lo : lo + n], window[:].bitcast(dt).indirect(lst[:, lo // 16 : (lo + n) // 16]))

        def move_plane(a):
            w0 = (a - 1) * S // 4
            for r in range(4):
                nc.sync.dma_start(v_sc_moved[r:P:32, w0 : w0 + S // 4], v_sc[8 * r + 3 + a : P : 32, :].bitcast(I32))

        def gather_cand(first, count, t):
            nc.vector.tensor_copy(t[:], tab2[:].bitcast(U32).indirect(idx2[:, 8 * first : 8 * (first + count)]))
            for n in range(count):
                cand[first + n] = t[:, P * n : P * (n + 1)]

        def v_words(a, jt):
            return v[a][:, P * jt : P * (jt + 1)].bitcast(FP8X4)

        def v_scale(a, jt):
            if a == 0:
                return v_sc[:, P * jt : P * (jt + 1)]
            c0 = (a - 1) * S + P * jt
            return v_sc_moved[:].bitcast(U8)[:, c0 : c0 + P]

        b_ps = [bank(jt, [P, H], "b%d" % jt) for jt in range(8)]
        sig = [kept([P, H], F32, "sig%d" % jt) for jt in range(EARLY)]
        sig.extend(
            shared.tile([P, H], F32, name="sig%d" % jt, offset=(4 + 2 * (jt - EARLY)) * KB, align_bytes=64) for jt in range(EARLY, 8)
        )

        def permuted(ps):
            return ps[:].rearrange("p (q u e) -> p u q e", u=2, e=2)

        def in_runs(t):
            return t[:].rearrange("p (u q e) -> p u q e", u=2, e=2)

        def b_pass(a, jts):
            for jt in jts:
                nc.tensor.matmul_mx(
                    b_ps[jt][:],
                    lhsT=v_words(a, jt),
                    lhsT_scale=v_scale(a, jt),
                    rhs=w4[:, a, :].bitcast(U8).bitcast(FP4X4),
                    rhs_scale=w4_sc[:].bitcast(U8)[:, H * a : H * (a + 1)],
                    start=(a == 0),
                    stop=(a == PASSES - 1),
                )

        def sigmoid(jts):
            for jt in jts:
                nc.scalar.activation(in_runs(sig[jt]), permuted(b_ps[jt]), ACT.Sigmoid)

        w1_grp = [kept([P, H, 4], BF16, "w1_grp%d" % a) for a in range(PASSES)]
        w1_sc = kept([P, PASSES, H], U8, "w1_sc")

        def round_by_copy(a, c0, c1, copy):
            copy(
                w1_grp[a][:, c0:c1, :].rearrange("p (c m) i -> p c i m", m=4),
                w1_raw[a][:, :, c0:c1].rearrange("p i (c m) -> p c i m", m=4),
            )

        w1_q = {}

        def quantize_w1(a, dst, cols=slice(0, H)):
            w1_q[a] = dst
            nc.vector.quantize_mx(dst[:, cols].bitcast(FP8X4), w1_sc[:, a, cols], w1_grp[a][:, cols, :].rearrange("p c i -> p (c i)"))

        a_ps = {}

        def a_pass(a, jt, cols=slice(0, H)):
            if a == 0:
                a_ps[jt] = bank(jt, [P, H], "a%d" % jt)
            nc.tensor.matmul_mx(
                a_ps[jt][:, cols],
                lhsT=v_words(a, jt),
                lhsT_scale=v_scale(a, jt),
                rhs=w1_q[a][:, cols].bitcast(FP8X4),
                rhs_scale=w1_sc[:, a, cols],
                start=(a == 0),
                stop=(a == PASSES - 1 and cols.stop == H),
            )

        lo_j, hi_j = range(0, 4), range(4, 8)
        gather(v2_sc, tab2_sc, idx2, U8, 0, S2)
        gather(v_sc, tab_sc, idx, U8, 0, S)
        move_plane(1)
        w1_raw = [load_w1(0, kept([P, 4, H], F32, "w1_raw0"))]
        move_plane(2)
        w1_raw.append(load_w1(1, kept([P, 4, H], F32, "w1_raw1")))
        w1_raw.append(load_w1(2, shared.tile([P, 4, H], F32, name="w1_raw2", offset=4 * KB, align_bytes=64)))
        tab2 = load_words(tab2_words[0], T2, "tab2")
        for r in range(4):
            nc.sync.dma_start(v2_sc_moved[r:P:32, :], v2_sc[8 * r : P : 32, :].bitcast(I32))
        cost_col = keep.tile([P, S2 // P], F32, name="cost_col")
        with nc.allow_non_contiguous_dma(reason="one cost a partition and candidate tile"):
            nc.sync.dma_start(cost_col[:], cost.rearrange("(t p) -> p t", p=P))

        for a in range(PASSES):
            gather(v[a], tab[a], idx, U32, 0, HALF)
            b_pass(a, lo_j)
            gather(v[a], tab[a], idx, U32, HALF, HALF)
            b_pass(a, hi_j)
        round_by_copy(0, 0, SCALAR_COLS[0], nc.scalar.copy)
        sigmoid(range(EARLY))
        halves = (slice(0, H // 2), slice(H // 2, H))
        round_by_copy(0, SCALAR_COLS[0], H, nc.vector.tensor_copy)
        quantize_w1(0, kept([P, H], U32, "w1_q0"))
        for jt in range(EARLY):
            a_pass(0, jt)
        for cols in halves:
            round_by_copy(1, cols.start, cols.stop, nc.vector.tensor_copy)
        w1_q1 = kept([P, H], U32, "w1_q1")
        for cols in halves:
            quantize_w1(1, w1_q1, cols)
        for jt in range(EARLY):
            a_pass(1, jt)
        for cols in halves:
            round_by_copy(2, cols.start, cols.start + SCALAR_COLS[2], nc.scalar.copy)
            round_by_copy(2, cols.start + SCALAR_COLS[2], cols.stop, nc.vector.tensor_copy)
        w1_q2 = kept([P, H], U32, "w1_q2")
        for cols in halves:
            quantize_w1(2, w1_q2, cols)
        sigmoid(range(EARLY, 8))
        for jt in lo_j:
            for cols in halves:
                a_pass(2, jt, cols)

        h_grp = [shared.tile([P, HALF, 4], BF16, name="h_grp0", offset=12 * KB, align_bytes=64), shared.tile([P, HALF, 4], BF16, name="h_grp1", offset=30 * KB, align_bytes=64)]
        h_q = [kept([P, HALF], U32, "h_q0"), shared.tile([P, HALF], U32, name="h_q1", offset=34 * KB, align_bytes=64)]
        h_sc = kept([P, S], U8, "h_sc")

        h_t = {}
        h_t_at = {6: 13 * KB, 7: 18 * KB}

        def gate(jt):
            if jt in h_t_at:
                h_t[jt] = shared.tile([P, H], BF16, name="h_t%d" % jt, offset=h_t_at[jt], align_bytes=64)
            else:
                h_t[jt] = kept([P, H], BF16, "h_t%d" % jt)
            nc.vector.tensor_tensor(in_runs(h_t[jt]), permuted(a_ps[jt]), in_runs(sig[jt]), ALU.mult)

        def gate_on_gpsimd(jt):
            a_sb = kept([P, H], F32, "a_sb%d" % jt)
            h_t[jt] = kept([P, H], BF16, "h_t%d" % jt)
            nc.scalar.copy(in_runs(a_sb), permuted(a_ps[jt]))
            nc.gpsimd.tensor_tensor(h_t[jt][:], a_sb[:], sig[jt][:], ALU.mult)

        def turn(first, count, bk, copy=nc.scalar.copy):
            ps = bank(bk, [P, count, 2, P], "h_ps%d" % first)
            for n in range(count):
                for u in range(2):
                    nc.tensor.transpose(ps[:, n, u, :], h_t[first + n][:].bitcast(F32)[:, P * u : P * (u + 1)], ident[:])
            cols = slice(P * (first % 4), P * (first % 4 + count))
            copy(
                h_grp[first // 4][:, cols, :].rearrange("p j t -> p (j t)").bitcast(F32).rearrange("p (n j u) -> p n j u", n=count, u=2),
                ps[:].rearrange("p n u j -> p n j u"),
            )

        def quantize_h(half):
            cols = slice(HALF * half, HALF * (half + 1))
            nc.vector.quantize_mx(h_q[half][:].bitcast(FP8X4), h_sc[:, cols], h_grp[half][:].rearrange("p j t -> p (j t)"))

        res = [keep.tile([P, S], F32, name="res%d" % it) for it in range(8)]

        mag_at = {1: 18 * KB, 4: 34 * KB}

        def edge_and_store(it, half, bk, pieces=1):
            cols = slice(HALF * half, HALF * (half + 1))
            z = bank(bk, [P, HALF], "z%d_%d" % (it, half))
            nc.tensor.matmul_mx(
                z[:],
                lhsT=cand[it].bitcast(FP8X4),
                lhsT_scale=v2_sc_moved[:].bitcast(U8)[:, P * it : P * (it + 1)],
                rhs=h_q[half][:].bitcast(FP8X4),
                rhs_scale=h_sc[:, cols],
                start=True,
                stop=True,
            )
            if half == 0 and it in mag_at:
                mag = shared.tile([P, HALF], F32, name="mag_first%d" % it, offset=mag_at[it], align_bytes=64)
            else:
                mag = work.tile([P, HALF], F32, tag="mag", name="mag%d_%d" % (it, half))
            width = HALF // pieces
            for c0 in range(0, HALF, width):
                part = slice(cols.start + c0, cols.start + c0 + width)
                nc.scalar.activation(mag[:, c0 : c0 + width], z[:, c0 : c0 + width], ACT.Abs)
                nc.vector.tensor_scalar(res[it][:, part], mag[:, c0 : c0 + width], cost_col[:, it : it + 1], 0.0, ALU.subtract, ALU.max)
                store(it, part)

        def store(it, cols):
            nc.sync.dma_start(out[P * it : P * (it + 1), cols], res[it][:, cols])

        gate(0)
        gate(1)
        for a in range(PASSES):
            a_pass(a, 4)
        gate_on_gpsimd(4)
        turn(0, 2, 0)
        gate(2)
        turn(2, 1, 5)
        gate(3)
        turn(3, 1, 6)
        for jt in range(5, 7):
            for a in range(PASSES):
                a_pass(a, jt)
        gather_cand(0, 4, kept([P, 4 * P], U32, "cand0"))
        quantize_h(0)
        gate_on_gpsimd(5)
        gather_cand(4, 4, shared.tile([P, 4 * P], U32, name="cand4", offset=14 * KB, align_bytes=64))
        gate(6)
        edge_and_store(0, 0, 7)
        for a in range(PASSES):
            a_pass(a, 7)
        edge_and_store(1, 0, 1)
        turn(4, 2, 1)
        gate(7)
        edge_and_store(2, 0, 2)
        turn(6, 1, 2, nc.vector.tensor_copy)
        edge_and_store(3, 0, 3)
        turn(7, 1, 5, nc.vector.tensor_copy)
        edge_and_store(4, 0, 0)
        quantize_h(1)
        for it in range(5, 8):
            edge_and_store(it, 0, (4, 6, 3)[it - 5])
        for it in range(8):
            edge_and_store(it, 1, (7, 1, 2, 5, 0, 4, 6, 3)[it], 2 if it == 7 else 1)
